import numpy as np
import ml_dtypes


def mxq(x, axis, fmt="e4m3"):
    dtype, down = {"e4m3": (ml_dtypes.float8_e4m3fn, 7), "e5m2": (ml_dtypes.float8_e5m2, 14)}[fmt]
    v = np.moveaxis(np.asarray(x, np.float32).astype(ml_dtypes.bfloat16).astype(np.float64), axis, -1)
    blocks = v.reshape(v.shape[:-1] + (-1, 32))
    amax = np.abs(blocks).max(-1, keepdims=True)
    byte = np.maximum(np.where(amax > 0, np.frexp(amax)[1] - 1 + 127, 0) - down, 1)
    scale = np.exp2(byte - 127.0)
    codes = (blocks / scale).astype(np.float32).astype(dtype).astype(np.float64)
    return np.moveaxis((codes * scale).reshape(v.shape), -1, axis)


WIDE = False


def mx_kscale(k):
    if not WIDE:
        return np.ones(k)
    levels = np.array([10, -10, 5, -5, 0])
    if k % 512:
        return np.exp2(np.random.permutation(np.resize(levels, k // 32))).repeat(32)
    a = np.empty((k // 512, 16))
    for p in range(k // 512):
        a[p, :8] = np.random.permutation(np.resize(levels, 8))
        for g in range(8):
            far = levels[np.abs(levels - a[p, g]) >= 10]
            a[p, g + 8] = far[np.random.randint(len(far))]
    return np.exp2(a.ravel()).repeat(32)


def f64(x):
    return np.asarray(x).astype(np.float64)


def striped(idx):
    return np.tile(idx.reshape(-1, 16).T, (8, 1)).astype(np.uint16)


def unstriped(offs):
    return offs[:16].T.reshape(-1).astype(np.int64)


def striped8(idx):
    return np.concatenate([x.reshape(-1, 16).T for x in idx]).astype(np.uint16)


def runs(offs, k):
    lists = np.stack([offs[16 * r : 16 * r + 16].T.reshape(-1) for r in range(8)]).astype(np.int64)
    return lists[np.arange(k) % 512 // 64]


def pack_weight(w):
    k, n = w.shape
    w = f64(np.asarray(w, np.float32).astype(ml_dtypes.bfloat16)).reshape(k // 32, 32, n)
    amax = np.abs(w).max(1)
    byte = np.clip(np.where(amax > 0, np.frexp(amax)[1] - 1 + 127 - 7, 1), 1, 254)
    scaled = (w * np.exp2(127.0 - byte)[:, None, :]).reshape(k, n).astype(np.float32)
    words = np.ascontiguousarray(scaled.reshape(k // 512, 128, 4, n).transpose(0, 1, 3, 2)).astype(ml_dtypes.float8_e4m3fn).view(np.uint8)
    return words, np.ascontiguousarray(byte.astype(np.uint8).reshape(k // 512, 16, n))


def unpack_weight(words, scales):
    g, p, n, _ = words.shape
    vals = np.ascontiguousarray(words).view(ml_dtypes.float8_e4m3fn).astype(np.float64) * np.repeat(np.exp2(scales.astype(np.float64) - 127.0), 8, axis=1)[..., None]
    return vals.transpose(0, 1, 3, 2).reshape(g * 512, n)


K, T, S, N, H = 1024, 2048, 512, 512, 512


def setup_inputs():
    n = np.random.standard_normal
    s = mx_kscale(K)[:, None]
    u = mx_kscale(H)
    packed_xT = pack_weight(n((K, T)) * s)
    return {
        "x_words": packed_xT[0],
        "x_scales": packed_xT[1],
        "w1": (n((K, H)) / np.sqrt(K) / s * u).astype(np.float32),
        "w2": (n((H, N)) / np.sqrt(H) / u[:, None]).astype(np.float32),
        "offs": striped(np.random.permutation(T)[:S]),
        "p1": striped8(np.stack([np.random.permutation(S) for _ in range(8)])),
        "p2": striped8(np.stack([np.random.permutation(S) for _ in range(8)])),
        "q1": striped8(np.stack([np.random.permutation(S) for _ in range(8)])),
        "q2": striped8(np.stack([np.random.permutation(S) for _ in range(8)])),
    }


def reference(x_words, x_scales, w1, w2, offs, p1, p2, q1, q2):
    xq = unpack_weight(x_words, x_scales)[:, unstriped(offs)]
    y = mxq(f64(w1), 0, "e4m3").T @ xq
    h = np.minimum(np.minimum(y, y[np.arange(H)[:, None], runs(p1, H)]), y[np.arange(H)[:, None], runs(p2, H)])
    z = np.maximum(np.maximum(h, h[np.arange(H)[:, None], runs(q1, H)]), h[np.arange(H)[:, None], runs(q2, H)])
    return mxq(f64(w2), 0, "e4m3").T @ mxq(z, 0, "e4m3")

@@ -1,0 +1,197 @@
+from contextlib import ExitStack
+
+import concourse.mybir as mybir
+
+K, T, S, N, H = 1024, 2048, 512, 512, 512
+FLOPS = 2 * K * H * S + 2 * H * N * S
+
+F32 = mybir.dt.float32
+BF16 = mybir.dt.bfloat16
+I32 = mybir.dt.int32
+U32 = mybir.dt.uint32
+U16 = mybir.dt.uint16
+U8 = mybir.dt.uint8
+FP8X4 = mybir.dt.float8_e4m3fn_x4
+MIN = mybir.AluOpType.min
+MAX = mybir.AluOpType.max
+
+P = 128
+PACK = 4
+K_PASS = P * PACK
+PASSES = K // K_PASS
+HALF = S // 2
+LIST = 16
+WIDE = 2 * S
+CHUNKS = ((0, 256), (256, 128), (384, 128))
+
+
+def tile_picked_opening_none_p_kernel(tc, x_words, x_scales, w1, w2, offs, p1, p2, q1, q2, out):
+    nc = tc.nc
+    with ExitStack() as ctx:
+        lists = ctx.enter_context(tc.tile_pool(name="lists", bufs=1))
+        keep = ctx.enter_context(tc.tile_pool(name="keep", bufs=1))
+        psum = ctx.enter_context(tc.psum_pool(name="psum", bufs=1))
+
+        def held(shape, dtype, name):
+            return keep.tile(shape, dtype, name=name, align_bytes=64)
+
+        def shared(shape, dtype, name, tag):
+            return keep.tile(shape, dtype, name=name, tag=tag, align_bytes=64)
+
+        def list_tile(name):
+            return lists.tile([P, S // LIST], U16, name=name)
+
+        offs_sb, p1_sb, p2_sb, q1_sb, q2_sb = [list_tile(name) for name in ("offs_sb", "p1_sb", "p2_sb", "q1_sb", "q2_sb")]
+        banks = [psum.tile([P, S], F32, name="bank%d" % b) for b in range(8)]
+
+        w1_raw = [held([P, PACK, H], F32, "w1_raw%d" % g) for g in range(PASSES)]
+        x_table = [held([P, T], U32, "x_table%d" % g) for g in range(PASSES)]
+        scale_table = held([P, T], U8, "scale_table")
+        w2_raw = held([P, PACK, N], F32, "w2_raw")
+
+        def load_w1(g):
+            nc.sync.dma_start(out=w1_raw[g][:], in_=w1[g * K_PASS : (g + 1) * K_PASS, :].rearrange("(p j) c -> p j c", j=PACK))
+
+        def load_x(g):
+            nc.sync.dma_start(out=x_table[g][:].bitcast(I32), in_=x_words[g].rearrange("p n t -> p (n t)").bitcast(I32))
+
+        nc.vector.memset(scale_table[:].bitcast(I32), 0)
+        load_w1(0)
+        for q in range(4):
+            nc.sync.dma_start(
+                out=scale_table[32 * q : 32 * q + 4 * PASSES, :].bitcast(I32),
+                in_=x_scales[:, 4 * q : 4 * q + 4, :].bitcast(I32),
+            )
+        nc.sync.dma_start(offs_sb[:], offs)
+        load_w1(1)
+        load_x(0)
+        load_x(1)
+        nc.sync.dma_start(p1_sb[:], p1)
+        nc.sync.dma_start(p2_sb[:], p2)
+        nc.sync.dma_start(out=w2_raw[:], in_=w2.rearrange("(p j) n -> p j n", j=PACK))
+        nc.sync.dma_start(q1_sb[:], q1)
+        nc.sync.dma_start(q2_sb[:], q2)
+
+        x_scale = held([P, S], U8, "x_scale")
+        nc.vector.tensor_copy(x_scale[:], scale_table[:].indirect(offs_sb[:]))
+
+        w1_codes, w1_scale = [], []
+        for g in range(PASSES):
+            grouped = held([P, PACK * H], BF16, "w1_grouped%d" % g)
+            dst = grouped[:].rearrange("p (t m j) -> p m t j", t=PACK, j=PACK)
+            src = w1_raw[g][:].rearrange("p j (m t) -> p m t j", t=PACK)
+            if g == 0:
+                nc.scalar.copy(dst, src)
+            else:
+                nc.vector.tensor_copy(dst, src)
+            codes = held([P, H], U32, "w1_codes%d" % g)
+            scale = held([P, H], U8, "w1_scale%d" % g)
+            nc.vector.quantize_mx(out=codes[:].bitcast(FP8X4), scales=scale[:], in_=grouped[:])
+            w1_codes.append(codes)
+            w1_scale.append(scale)
+
+        x_codes = [held([P, S], U32, "x_codes%d" % g) for g in range(PASSES)]
+        nc.vector.tensor_copy(x_codes[0][:], x_table[0][:].indirect(offs_sb[:]))
+
+        def first_product(acc, t, g, cols):
+            nc.tensor.matmul_mx(
+                out=acc,
+                lhsT=w1_codes[g][:, t * P : (t + 1) * P].bitcast(FP8X4),
+                lhsT_scale=w1_scale[g][:, t * P : (t + 1) * P],
+                rhs=x_codes[g][:, cols].bitcast(FP8X4),
+                rhs_scale=x_scale[4 * g : P, cols],
+                start=(g == 0),
+                stop=(g == PASSES - 1),
+            )
+
+        halves = (slice(0, HALF), slice(HALF, S))
+        pieces = [(banks[u][:, 0:HALF], 0, halves[u]) for u in range(2)]
+        pieces = pieces + [(banks[1 + t][:], t, slice(0, S)) for t in range(1, PACK)]
+        for acc, t, cols in pieces:
+            first_product(acc, t, 0, cols)
+        for u in range(2):
+            nc.vector.tensor_copy(
+                x_codes[1][:, halves[u]],
+                x_table[1][:].indirect(offs_sb[:, u * HALF // LIST : (u + 1) * HALF // LIST]),
+            )
+        y = [held([P, WIDE], F32, "y%d" % t) for t in range(PACK)]
+        for acc, t, cols in pieces:
+            first_product(acc, t, 1, cols)
+            nc.scalar.copy(y[t][:, cols], acc)
+
+        w2_grouped = held([P, PACK * N], BF16, "w2_grouped")
+        nc.scalar.copy(
+            w2_grouped[:].rearrange("p (c i j) -> p c j i", i=4, j=PACK),
+            w2_raw[:].rearrange("p j (c i) -> p c j i", i=4),
+        )
+
+        h = [held([P, S], F32, "h%d" % t) for t in range(PACK)]
+        h_round = held([P, PACK, S], BF16, "h_round")
+        for t in range(PACK):
+            near1 = held([P, S], F32, "near1_%d" % t)
+            near2 = held([P, S], F32, "near2_%d" % t)
+            nc.vector.tensor_copy(near1[:], y[t][:].indirect(p1_sb[:]))
+            nc.vector.tensor_copy(near2[:], y[t][:].indirect(p2_sb[:]))
+            least = held([P, S], F32, "least%d" % t)
+            nc.vector.tensor_tensor(least[:], near1[:], y[t][:, 0:S], MIN)
+            nc.vector.tensor_tensor(h[t][:], least[:], near2[:], MIN)
+            nc.scalar.copy(h_round[:, t, :], h[t][:])
+
+        w2_codes = held([P, N], U32, "w2_codes")
+        w2_scale = held([P, N], U8, "w2_scale")
+        nc.vector.quantize_mx(out=w2_codes[:].bitcast(FP8X4), scales=w2_scale[:], in_=w2_grouped[:])
+
+        out_view = out.rearrange("(a p) j -> p a j", p=P)
+        chunk_banks = ((5, 6), (7,), (0, 1))
+        for c, (c0, width) in enumerate(CHUNKS):
+            last = c == len(CHUNKS) - 1
+            entries = slice(c0 // LIST, (c0 + width) // LIST)
+            far1 = shared([P, PACK, width], BF16, "far1_%d" % c, "zg%d" % (c - 2) if c >= 2 else "far1_%d" % c)
+            far2 = shared([P, PACK, width], BF16, "far2_%d" % c, "zp%d" % (c - 1) if c >= 1 else "far2_%d" % c)
+            most = held([P, PACK, width], BF16, "most%d" % c)
+            z = shared([P, PACK, width], BF16, "z%d" % c, "zp%d" % c)
+            for t in range(PACK):
+                nc.vector.tensor_copy(far1[:, t, :], h[t][:].indirect(q1_sb[:, entries]))
+            for t in range(PACK):
+                nc.vector.tensor_copy(far2[:, t, :], h[t][:].indirect(q2_sb[:, entries]))
+                if t == 0:
+                    nc.vector.tensor_tensor(most[:], far1[:], h_round[:, :, c0 : c0 + width], MAX)
+            z_grouped = shared([P, PACK * width], BF16, "z_grouped%d" % c, "zg%d" % c)
+            dst = z_grouped[:].rearrange("p (c i t) -> p c t i", i=4, t=PACK)
+            src = z[:].rearrange("p t (c i) -> p c t i", i=4)
+            if last:
+                nc.vector.tensor_tensor(z[:, 0:3, :], most[:, 0:3, :], far2[:, 0:3, :], MAX)
+                nc.vector.tensor_tensor(z[:, 3, :], most[:, 3, :], far2[:, 3, :], MAX)
+                nc.vector.tensor_copy(dst, src)
+            else:
+                nc.vector.tensor_tensor(z[:], most[:], far2[:], MAX)
+                nc.scalar.copy(dst, src)
+            z_codes = held([P, width], U32, "z_codes%d" % c)
+            z_scale = held([P, width], U8, "z_scale%d" % c)
+            nc.vector.quantize_mx(out=z_codes[:].bitcast(FP8X4), scales=z_scale[:], in_=z_grouped[:])
+
+            result = held([P, N // P, width], F32, "result%d" % c)
+            per_bank = (N // P) // len(chunk_banks[c])
+            for b, bank in enumerate(chunk_banks[c]):
+                for a in range(per_bank):
+                    m = b * per_bank + a
+                    nc.tensor.matmul_mx(
+                        out=banks[bank][:, a * width : (a + 1) * width],
+                        lhsT=w2_codes[:, m * P : (m + 1) * P].bitcast(FP8X4),
+                        lhsT_scale=w2_scale[:, m * P : (m + 1) * P],
+                        rhs=z_codes[:].bitcast(FP8X4),
+                        rhs_scale=z_scale[:],
+                        start=True,
+                        stop=True,
+                    )
+                rows = slice(b * per_bank, (b + 1) * per_bank)
+                staged = result[:, rows, :].rearrange("p a j -> p (a j)")
+                if last and b == 1:
+                    nc.vector.tensor_copy(staged, banks[bank][:, 0 : per_bank * width])
+                else:
+                    nc.scalar.copy(staged, banks[bank][:, 0 : per_bank * width])
+                if last:
+                    queue = nc.scalar if b == 0 else nc.sync
+                    queue.dma_start(out=out_view[:, rows, c0 : c0 + width], in_=result[:, rows, :])
+            if not last:
+                nc.sync.dma_start(out=out_view[:, :, c0 : c0 + width], in_=result[:])

@@ -143,33 +143,72 @@ def tile_picked_opening_none_p_kernel(tc, x_words, x_scales, w1, w2, offs, p1, p
 
         out_view = out.rearrange("(a p) j -> p a j", p=P)
         chunk_banks = ((5, 6), (7,), (0, 1))
-        for c, (c0, width) in enumerate(CHUNKS):
+        early_tags = ("early0", "late1_0", "zg0")
+        late1_tags = ("late1_0", "early0", "zp0")
+        late2_tags = ("late2_0", "zp0", "zp1")
+        far1, far2, early, late1, late2, most, z, z_grouped = [], [], [], [], [], [], [], []
+
+        def open_chunk(c):
+            width = CHUNKS[c][1]
+            early.append(shared([P, 4, width], BF16, "early%d" % c, early_tags[c]))
+
+        def open_late1(c):
+            width = CHUNKS[c][1]
+            late1.append(shared([P, 2, width], BF16, "late1_%d" % c, late1_tags[c]))
+            most.append(held([P, PACK, width], BF16, "most%d" % c))
+
+        def open_late2(c):
+            width = CHUNKS[c][1]
+            late2.append(shared([P, 2, width], BF16, "late2_%d" % c, late2_tags[c]))
+
+        def open_z(c):
+            width = CHUNKS[c][1]
+            z.append(shared([P, PACK, width], BF16, "z%d" % c, "zp%d" % c))
+
+        def entries(c):
+            c0, width = CHUNKS[c]
+            return slice(c0 // LIST, (c0 + width) // LIST)
+
+        def fetch1(c, t):
+            dst = early[c][:, t, :] if t < 2 else late1[c][:, t - 2, :]
+            nc.vector.tensor_copy(dst, h[t][:].indirect(q1_sb[:, entries(c)]))
+
+        def fetch2(c, t):
+            dst = early[c][:, 2 + t, :] if t < 2 else late2[c][:, t - 2, :]
+            nc.vector.tensor_copy(dst, h[t][:].indirect(q2_sb[:, entries(c)]))
+
+        def first_max(c, u):
+            c0, width = CHUNKS[c]
+            src = early[c][:, 0:2, :] if u == 0 else late1[c][:]
+            nc.vector.tensor_tensor(most[c][:, 2 * u : 2 * u + 2, :], src, h_round[:, 2 * u : 2 * u + 2, c0 : c0 + width], MAX)
+
+        def second_max(c, t0, t1):
+            src = early[c][:, 2 + t0 : 2 + t1, :] if t0 < 2 else late2[c][:, t0 - 2 : t1 - 2, :]
+            nc.vector.tensor_tensor(z[c][:, t0:t1, :], most[c][:, t0:t1, :], src, MAX)
+
+        def woven_max(c, u):
+            src = early[c][:, 2:4, :] if u == 0 else late2[c][:]
+            nc.vector.tensor_tensor(
+                z_grouped[c][:].rearrange("p (c t) -> p c t", t=PACK)[:, :, 2 * u : 2 * u + 2],
+                most[c][:, 2 * u : 2 * u + 2, :].rearrange("p t c -> p c t"),
+                src.rearrange("p t c -> p c t"),
+                MAX,
+            )
+
+        def weave(c, copy):
+            width = CHUNKS[c][1]
+            z_grouped.append(shared([P, PACK * width], BF16, "z_grouped%d" % c, "zg%d" % c))
+            copy(
+                z_grouped[c][:].rearrange("p (c i t) -> p c t i", i=4, t=PACK),
+                z[c][:].rearrange("p t (c i) -> p c t i", i=4),
+            )
+
+        def second_product(c):
+            c0, width = CHUNKS[c]
             last = c == len(CHUNKS) - 1
-            entries = slice(c0 // LIST, (c0 + width) // LIST)
-            far1 = shared([P, PACK, width], BF16, "far1_%d" % c, "zg%d" % (c - 2) if c >= 2 else "far1_%d" % c)
-            far2 = shared([P, PACK, width], BF16, "far2_%d" % c, "zp%d" % (c - 1) if c >= 1 else "far2_%d" % c)
-            most = held([P, PACK, width], BF16, "most%d" % c)
-            z = shared([P, PACK, width], BF16, "z%d" % c, "zp%d" % c)
-            for t in range(PACK):
-                nc.vector.tensor_copy(far1[:, t, :], h[t][:].indirect(q1_sb[:, entries]))
-            for t in range(PACK):
-                nc.vector.tensor_copy(far2[:, t, :], h[t][:].indirect(q2_sb[:, entries]))
-                if t == 0:
-                    nc.vector.tensor_tensor(most[:], far1[:], h_round[:, :, c0 : c0 + width], MAX)
-            z_grouped = shared([P, PACK * width], BF16, "z_grouped%d" % c, "zg%d" % c)
-            dst = z_grouped[:].rearrange("p (c i t) -> p c t i", i=4, t=PACK)
-            src = z[:].rearrange("p t (c i) -> p c t i", i=4)
-            if last:
-                nc.vector.tensor_tensor(z[:, 0:3, :], most[:, 0:3, :], far2[:, 0:3, :], MAX)
-                nc.vector.tensor_tensor(z[:, 3, :], most[:, 3, :], far2[:, 3, :], MAX)
-                nc.vector.tensor_copy(dst, src)
-            else:
-                nc.vector.tensor_tensor(z[:], most[:], far2[:], MAX)
-                nc.scalar.copy(dst, src)
             z_codes = held([P, width], U32, "z_codes%d" % c)
             z_scale = held([P, width], U8, "z_scale%d" % c)
-            nc.vector.quantize_mx(out=z_codes[:].bitcast(FP8X4), scales=z_scale[:], in_=z_grouped[:])
-
+            nc.vector.quantize_mx(out=z_codes[:].bitcast(FP8X4), scales=z_scale[:], in_=z_grouped[c][:])
             result = held([P, N // P, width], F32, "result%d" % c)
             per_bank = (N // P) // len(chunk_banks[c])
             for b, bank in enumerate(chunk_banks[c]):
@@ -195,3 +234,43 @@ def tile_picked_opening_none_p_kernel(tc, x_words, x_scales, w1, w2, offs, p1, p
                     queue.dma_start(out=out_view[:, rows, c0 : c0 + width], in_=result[:, rows, :])
             if not last:
                 nc.sync.dma_start(out=out_view[:, :, c0 : c0 + width], in_=result[:])
+
+        open_chunk(0)
+        open_late1(0)
+        open_late2(0)
+        open_z(0)
+        for t in range(PACK):
+            fetch1(0, t)
+        fetch2(0, 0)
+        first_max(0, 0)
+        fetch2(0, 1)
+        first_max(0, 1)
+        fetch2(0, 2)
+        second_max(0, 0, 2)
+        fetch2(0, 3)
+        for c in range(1, len(CHUNKS)):
+            open_chunk(c)
+            fetch1(c, 0)
+            second_max(c - 1, 2, 4)
+            weave(c - 1, nc.scalar.copy)
+            fetch1(c, 1)
+            fetch2(c, 0)
+            open_late1(c)
+            first_max(c, 0)
+            fetch2(c, 1)
+            fetch1(c, 2)
+            if c == len(CHUNKS) - 1:
+                z_grouped.append(held([P, PACK * CHUNKS[c][1]], BF16, "z_grouped_last"))
+                woven_max(c, 0)
+            else:
+                open_z(c)
+                second_max(c, 0, 2)
+            fetch1(c, 3)
+            second_product(c - 1)
+            open_late2(c)
+            first_max(c, 1)
+            fetch2(c, 2)
+            fetch2(c, 3)
+        c = len(CHUNKS) - 1
+        woven_max(c, 1)
+        second_product(c)

@@ -17,12 +17,19 @@ MAX = mybir.AluOpType.max
 
 P = 128
 PACK = 4
+PAIR = 2
 K_PASS = P * PACK
 PASSES = K // K_PASS
+QUADRANT = 32
+SCALE_ROWS = 4
+LIST_COLUMN = 16
+LINE = 4
 HALF = S // 2
-LIST = 16
-WIDE = 2 * S
+Y_WINDOW = 2 * S
 CHUNKS = ((0, 256), (256, 128), (384, 128))
+LAST = len(CHUNKS) - 1
+PSUM_BANKS = 8
+CHUNK_BANKS = ((6, 7), (3,), (4, 5))
 
 
 def tile_picked_opening_none_p_kernel(tc, x_words, x_scales, w1, w2, offs, p1, p2, q1, q2, out):
@@ -39,10 +46,13 @@ def tile_picked_opening_none_p_kernel(tc, x_words, x_scales, w1, w2, offs, p1, p
             return keep.tile(shape, dtype, name=name, tag=tag, align_bytes=64)
 
         def list_tile(name):
-            return lists.tile([P, S // LIST], U16, name=name)
+            return lists.tile([P, S // LIST_COLUMN], U16, name=name)
+
+        def entries(first, count):
+            return slice(first // LIST_COLUMN, (first + count) // LIST_COLUMN)
 
         offs_sb, p1_sb, p2_sb, q1_sb, q2_sb = [list_tile(name) for name in ("offs_sb", "p1_sb", "p2_sb", "q1_sb", "q2_sb")]
-        banks = [psum.tile([P, S], F32, name="bank%d" % b) for b in range(8)]
+        banks = [psum.tile([P, S], F32, name="bank%d" % b) for b in range(PSUM_BANKS)]
 
         w1_raw = [held([P, PACK, H], F32, "w1_raw%d" % g) for g in range(PASSES)]
         x_table = [held([P, T], U32, "x_table%d" % g) for g in range(PASSES)]
@@ -57,10 +67,10 @@ def tile_picked_opening_none_p_kernel(tc, x_words, x_scales, w1, w2, offs, p1, p
 
         nc.vector.memset(scale_table[:].bitcast(I32), 0)
         load_w1(0)
-        for q in range(4):
+        for q in range(P // QUADRANT):
             nc.sync.dma_start(
-                out=scale_table[32 * q : 32 * q + 4 * PASSES, :].bitcast(I32),
-                in_=x_scales[:, 4 * q : 4 * q + 4, :].bitcast(I32),
+                out=scale_table[QUADRANT * q : QUADRANT * q + SCALE_ROWS * PASSES, :].bitcast(I32),
+                in_=x_scales[:, SCALE_ROWS * q : SCALE_ROWS * (q + 1), :].bitcast(I32),
             )
         nc.sync.dma_start(offs_sb[:], offs)
         load_w1(1)
@@ -75,143 +85,145 @@ def tile_picked_opening_none_p_kernel(tc, x_words, x_scales, w1, w2, offs, p1, p
         x_scale = held([P, S], U8, "x_scale")
         nc.vector.tensor_copy(x_scale[:], scale_table[:].indirect(offs_sb[:]))
 
-        w1_codes, w1_scale = [], []
+        w1_codes, w1_scale = {}, {}
         for g in range(PASSES):
-            grouped = held([P, PACK * H], BF16, "w1_grouped%d" % g)
-            dst = grouped[:].rearrange("p (t m j) -> p m t j", t=PACK, j=PACK)
-            src = w1_raw[g][:].rearrange("p j (m t) -> p m t j", t=PACK)
-            if g == 0:
-                nc.scalar.copy(dst, src)
-            else:
-                nc.vector.tensor_copy(dst, src)
-            codes = held([P, H], U32, "w1_codes%d" % g)
-            scale = held([P, H], U8, "w1_scale%d" % g)
-            nc.vector.quantize_mx(out=codes[:].bitcast(FP8X4), scales=scale[:], in_=grouped[:])
-            w1_codes.append(codes)
-            w1_scale.append(scale)
+            dealt = w1_raw[g][:].rearrange("p j (m t) -> p m t j", t=PACK)
+            for u, copy in enumerate((nc.vector.tensor_copy, nc.scalar.copy)):
+                w1_woven = held([P, PAIR * P * PACK], BF16, "w1_woven%d_%d" % (g, u))
+                copy(w1_woven[:].rearrange("p (t m j) -> p m t j", t=PAIR, j=PACK), dealt[:, :, PAIR * u : PAIR * (u + 1), :])
+                codes = held([P, PAIR * P], U32, "w1_codes%d_%d" % (g, u))
+                scale = held([P, PAIR * P], U8, "w1_scale%d_%d" % (g, u))
+                nc.vector.quantize_mx(out=codes[:].bitcast(FP8X4), scales=scale[:], in_=w1_woven[:])
+                for e in range(PAIR):
+                    w1_codes[g, PAIR * u + e] = codes[:, e * P : (e + 1) * P]
+                    w1_scale[g, PAIR * u + e] = scale[:, e * P : (e + 1) * P]
 
         x_codes = [held([P, S], U32, "x_codes%d" % g) for g in range(PASSES)]
         nc.vector.tensor_copy(x_codes[0][:], x_table[0][:].indirect(offs_sb[:]))
 
-        def first_product(acc, t, g, cols):
+        def first_product(acc, t, g, cells):
             nc.tensor.matmul_mx(
                 out=acc,
-                lhsT=w1_codes[g][:, t * P : (t + 1) * P].bitcast(FP8X4),
-                lhsT_scale=w1_scale[g][:, t * P : (t + 1) * P],
-                rhs=x_codes[g][:, cols].bitcast(FP8X4),
-                rhs_scale=x_scale[4 * g : P, cols],
+                lhsT=w1_codes[g, t].bitcast(FP8X4),
+                lhsT_scale=w1_scale[g, t],
+                rhs=x_codes[g][:, cells].bitcast(FP8X4),
+                rhs_scale=x_scale[SCALE_ROWS * g : P, cells],
                 start=(g == 0),
                 stop=(g == PASSES - 1),
             )
 
-        halves = (slice(0, HALF), slice(HALF, S))
-        pieces = [(banks[u][:, 0:HALF], 0, halves[u]) for u in range(2)]
-        pieces = pieces + [(banks[1 + t][:], t, slice(0, S)) for t in range(1, PACK)]
-        for acc, t, cols in pieces:
-            first_product(acc, t, 0, cols)
-        for u in range(2):
-            nc.vector.tensor_copy(
-                x_codes[1][:, halves[u]],
-                x_table[1][:].indirect(offs_sb[:, u * HALF // LIST : (u + 1) * HALF // LIST]),
-            )
-        y = [held([P, WIDE], F32, "y%d" % t) for t in range(PACK)]
-        for acc, t, cols in pieces:
-            first_product(acc, t, 1, cols)
-            nc.scalar.copy(y[t][:, cols], acc)
+        pieces = [
+            (banks[0][:, 0:HALF], 0, slice(0, HALF)),
+            (banks[1][:, 0:P], 0, slice(HALF, HALF + P)),
+            (banks[5][:, 0:P], 0, slice(HALF + P, S)),
+            (banks[2][:], 1, slice(0, S)),
+        ]
+        for acc, t, cells in pieces:
+            first_product(acc, t, 0, cells)
+        for first in (0, HALF):
+            nc.vector.tensor_copy(x_codes[1][:, first : first + HALF], x_table[1][:].indirect(offs_sb[:, entries(first, HALF)]))
+        y = [held([P, Y_WINDOW], F32, "y%d" % t) for t in range(PACK)]
+        for acc, t, cells in pieces:
+            first_product(acc, t, 1, cells)
+            nc.scalar.copy(y[t][:, cells], acc)
+        for t in range(PAIR, PACK):
+            acc = banks[t - PAIR][:]
+            for g in range(PASSES):
+                first_product(acc, t, g, slice(0, S))
+            nc.scalar.copy(y[t][:, 0:S], acc)
 
-        w2_grouped = held([P, PACK * N], BF16, "w2_grouped")
+        w2_woven = held([P, PACK * N], BF16, "w2_woven")
         nc.scalar.copy(
-            w2_grouped[:].rearrange("p (c i j) -> p c j i", i=4, j=PACK),
-            w2_raw[:].rearrange("p j (c i) -> p c j i", i=4),
+            w2_woven[:].rearrange("p (c i j) -> p c j i", i=LINE, j=PACK),
+            w2_raw[:].rearrange("p j (c i) -> p c j i", i=LINE),
         )
 
         h = [held([P, S], F32, "h%d" % t) for t in range(PACK)]
         h_round = held([P, PACK, S], BF16, "h_round")
-        for t in range(PACK):
-            near1 = held([P, S], F32, "near1_%d" % t)
-            near2 = held([P, S], F32, "near2_%d" % t)
-            nc.vector.tensor_copy(near1[:], y[t][:].indirect(p1_sb[:]))
-            nc.vector.tensor_copy(near2[:], y[t][:].indirect(p2_sb[:]))
-            least = held([P, S], F32, "least%d" % t)
-            nc.vector.tensor_tensor(least[:], near1[:], y[t][:, 0:S], MIN)
-            nc.vector.tensor_tensor(h[t][:], least[:], near2[:], MIN)
+        near1 = [held([P, S], F32, "near1_%d" % t) for t in range(PACK)]
+        near2 = [held([P, S], F32, "near2_%d" % t) for t in range(PACK)]
+        least = [held([P, S], F32, "least%d" % t) for t in range(PACK)]
+
+        def second_min(t):
+            nc.vector.tensor_tensor(h[t][:], least[t][:], near2[t][:], MIN)
             nc.scalar.copy(h_round[:, t, :], h[t][:])
+
+        for t in range(PACK):
+            nc.vector.tensor_copy(near1[t][:], y[t][:].indirect(p1_sb[:]))
+            if t > 0:
+                second_min(t - 1)
+            nc.vector.tensor_copy(near2[t][:], y[t][:].indirect(p2_sb[:]))
+            nc.vector.tensor_tensor(least[t][:], near1[t][:], y[t][:, 0:S], MIN)
 
         w2_codes = held([P, N], U32, "w2_codes")
         w2_scale = held([P, N], U8, "w2_scale")
-        nc.vector.quantize_mx(out=w2_codes[:].bitcast(FP8X4), scales=w2_scale[:], in_=w2_grouped[:])
+        nc.vector.quantize_mx(out=w2_codes[:].bitcast(FP8X4), scales=w2_scale[:], in_=w2_woven[:])
+        second_min(PACK - 1)
 
+        low_tags = ("low0", "high1_0", "z_woven0")
+        high1_tags = ("high1_0", "low0", "z0")
+        high2_tags = ("high2_0", "z0", "z1")
+        low, high1, high2, most, z, z_woven = [], [], [], [], [], []
         out_view = out.rearrange("(a p) j -> p a j", p=P)
-        chunk_banks = ((5, 6), (7,), (0, 1))
-        early_tags = ("early0", "late1_0", "zg0")
-        late1_tags = ("late1_0", "early0", "zp0")
-        late2_tags = ("late2_0", "zp0", "zp1")
-        far1, far2, early, late1, late2, most, z, z_grouped = [], [], [], [], [], [], [], []
 
-        def open_chunk(c):
-            width = CHUNKS[c][1]
-            early.append(shared([P, 4, width], BF16, "early%d" % c, early_tags[c]))
+        def open_low(c):
+            low.append(shared([P, 2 * PAIR, CHUNKS[c][1]], BF16, "low%d" % c, low_tags[c]))
 
-        def open_late1(c):
-            width = CHUNKS[c][1]
-            late1.append(shared([P, 2, width], BF16, "late1_%d" % c, late1_tags[c]))
-            most.append(held([P, PACK, width], BF16, "most%d" % c))
+        def open_high1(c):
+            high1.append(shared([P, PAIR, CHUNKS[c][1]], BF16, "high1_%d" % c, high1_tags[c]))
+            most.append(held([P, PACK, CHUNKS[c][1]], BF16, "most%d" % c))
 
-        def open_late2(c):
-            width = CHUNKS[c][1]
-            late2.append(shared([P, 2, width], BF16, "late2_%d" % c, late2_tags[c]))
+        def open_high2(c):
+            high2.append(shared([P, PAIR, CHUNKS[c][1]], BF16, "high2_%d" % c, high2_tags[c]))
 
         def open_z(c):
-            width = CHUNKS[c][1]
-            z.append(shared([P, PACK, width], BF16, "z%d" % c, "zp%d" % c))
-
-        def entries(c):
-            c0, width = CHUNKS[c]
-            return slice(c0 // LIST, (c0 + width) // LIST)
+            z.append(shared([P, PACK, CHUNKS[c][1]], BF16, "z%d" % c, "z%d" % c))
 
         def fetch1(c, t):
-            dst = early[c][:, t, :] if t < 2 else late1[c][:, t - 2, :]
-            nc.vector.tensor_copy(dst, h[t][:].indirect(q1_sb[:, entries(c)]))
+            dst = low[c][:, t, :] if t < PAIR else high1[c][:, t - PAIR, :]
+            nc.vector.tensor_copy(dst, h[t][:].indirect(q1_sb[:, entries(*CHUNKS[c])]))
 
         def fetch2(c, t):
-            dst = early[c][:, 2 + t, :] if t < 2 else late2[c][:, t - 2, :]
-            nc.vector.tensor_copy(dst, h[t][:].indirect(q2_sb[:, entries(c)]))
+            dst = low[c][:, PAIR + t, :] if t < PAIR else high2[c][:, t - PAIR, :]
+            nc.vector.tensor_copy(dst, h[t][:].indirect(q2_sb[:, entries(*CHUNKS[c])]))
+
+        def pair(u):
+            return slice(PAIR * u, PAIR * (u + 1))
 
         def first_max(c, u):
-            c0, width = CHUNKS[c]
-            src = early[c][:, 0:2, :] if u == 0 else late1[c][:]
-            nc.vector.tensor_tensor(most[c][:, 2 * u : 2 * u + 2, :], src, h_round[:, 2 * u : 2 * u + 2, c0 : c0 + width], MAX)
+            first, width = CHUNKS[c]
+            by_q1 = low[c][:, pair(0), :] if u == 0 else high1[c][:]
+            nc.vector.tensor_tensor(most[c][:, pair(u), :], by_q1, h_round[:, pair(u), first : first + width], MAX)
 
-        def second_max(c, t0, t1):
-            src = early[c][:, 2 + t0 : 2 + t1, :] if t0 < 2 else late2[c][:, t0 - 2 : t1 - 2, :]
-            nc.vector.tensor_tensor(z[c][:, t0:t1, :], most[c][:, t0:t1, :], src, MAX)
+        def by_q2(c, u):
+            return low[c][:, pair(1), :] if u == 0 else high2[c][:]
+
+        def second_max(c, u):
+            nc.vector.tensor_tensor(z[c][:, pair(u), :], most[c][:, pair(u), :], by_q2(c, u), MAX)
 
         def woven_max(c, u):
-            src = early[c][:, 2:4, :] if u == 0 else late2[c][:]
             nc.vector.tensor_tensor(
-                z_grouped[c][:].rearrange("p (c t) -> p c t", t=PACK)[:, :, 2 * u : 2 * u + 2],
-                most[c][:, 2 * u : 2 * u + 2, :].rearrange("p t c -> p c t"),
-                src.rearrange("p t c -> p c t"),
+                z_woven[c][:].rearrange("p (c t) -> p c t", t=PACK)[:, :, pair(u)],
+                most[c][:, pair(u), :].rearrange("p t c -> p c t"),
+                by_q2(c, u).rearrange("p t c -> p c t"),
                 MAX,
             )
 
-        def weave(c, copy):
-            width = CHUNKS[c][1]
-            z_grouped.append(shared([P, PACK * width], BF16, "z_grouped%d" % c, "zg%d" % c))
-            copy(
-                z_grouped[c][:].rearrange("p (c i t) -> p c t i", i=4, t=PACK),
-                z[c][:].rearrange("p t (c i) -> p c t i", i=4),
+        def weave(c):
+            z_woven.append(shared([P, PACK * CHUNKS[c][1]], BF16, "z_woven%d" % c, "z_woven%d" % c))
+            nc.scalar.copy(
+                z_woven[c][:].rearrange("p (c i t) -> p c t i", i=LINE, t=PACK),
+                z[c][:].rearrange("p t (c i) -> p c t i", i=LINE),
             )
 
         def second_product(c):
-            c0, width = CHUNKS[c]
-            last = c == len(CHUNKS) - 1
+            first, width = CHUNKS[c]
             z_codes = held([P, width], U32, "z_codes%d" % c)
             z_scale = held([P, width], U8, "z_scale%d" % c)
-            nc.vector.quantize_mx(out=z_codes[:].bitcast(FP8X4), scales=z_scale[:], in_=z_grouped[c][:])
+            nc.vector.quantize_mx(out=z_codes[:].bitcast(FP8X4), scales=z_scale[:], in_=z_woven[c][:])
             result = held([P, N // P, width], F32, "result%d" % c)
-            per_bank = (N // P) // len(chunk_banks[c])
-            for b, bank in enumerate(chunk_banks[c]):
+            per_bank = (N // P) // len(CHUNK_BANKS[c])
+            for b, bank in enumerate(CHUNK_BANKS[c]):
                 for a in range(per_bank):
                     m = b * per_bank + a
                     nc.tensor.matmul_mx(
@@ -225,19 +237,19 @@ def tile_picked_opening_none_p_kernel(tc, x_words, x_scales, w1, w2, offs, p1, p
                     )
                 rows = slice(b * per_bank, (b + 1) * per_bank)
                 staged = result[:, rows, :].rearrange("p a j -> p (a j)")
-                if last and b == 1:
+                if c == LAST and b == 1:
                     nc.vector.tensor_copy(staged, banks[bank][:, 0 : per_bank * width])
                 else:
                     nc.scalar.copy(staged, banks[bank][:, 0 : per_bank * width])
-                if last:
+                if c == LAST:
                     queue = nc.scalar if b == 0 else nc.sync
-                    queue.dma_start(out=out_view[:, rows, c0 : c0 + width], in_=result[:, rows, :])
-            if not last:
-                nc.sync.dma_start(out=out_view[:, :, c0 : c0 + width], in_=result[:])
+                    queue.dma_start(out=out_view[:, rows, first : first + width], in_=result[:, rows, :])
+            if c != LAST:
+                nc.sync.dma_start(out=out_view[:, :, first : first + width], in_=result[:])
 
-        open_chunk(0)
-        open_late1(0)
-        open_late2(0)
+        open_low(0)
+        open_high1(0)
+        open_high2(0)
         open_z(0)
         for t in range(PACK):
             fetch1(0, t)
@@ -246,31 +258,30 @@ def tile_picked_opening_none_p_kernel(tc, x_words, x_scales, w1, w2, offs, p1, p
         fetch2(0, 1)
         first_max(0, 1)
         fetch2(0, 2)
-        second_max(0, 0, 2)
+        second_max(0, 0)
         fetch2(0, 3)
         for c in range(1, len(CHUNKS)):
-            open_chunk(c)
+            open_low(c)
             fetch1(c, 0)
-            second_max(c - 1, 2, 4)
-            weave(c - 1, nc.scalar.copy)
+            second_max(c - 1, 1)
+            weave(c - 1)
             fetch1(c, 1)
             fetch2(c, 0)
-            open_late1(c)
+            open_high1(c)
             first_max(c, 0)
             fetch2(c, 1)
             fetch1(c, 2)
-            if c == len(CHUNKS) - 1:
-                z_grouped.append(held([P, PACK * CHUNKS[c][1]], BF16, "z_grouped_last"))
+            if c == LAST:
+                z_woven.append(held([P, PACK * CHUNKS[c][1]], BF16, "z_woven_last"))
                 woven_max(c, 0)
             else:
                 open_z(c)
-                second_max(c, 0, 2)
+                second_max(c, 0)
             fetch1(c, 3)
             second_product(c - 1)
-            open_late2(c)
+            open_high2(c)
             first_max(c, 1)
             fetch2(c, 2)
             fetch2(c, 3)
-        c = len(CHUNKS) - 1
-        woven_max(c, 1)
-        second_product(c)
+        woven_max(LAST, 1)
+        second_product(LAST)

@@ -65,15 +65,21 @@ def tile_picked_opening_none_p_kernel(tc, x_words, x_scales, w1, w2, offs, p1, p
         def load_x(g):
             nc.sync.dma_start(out=x_table[g][:].bitcast(I32), in_=x_words[g].rearrange("p n t -> p (n t)").bitcast(I32))
 
+        def load_scale_rows(r):
+            for g in range(PASSES):
+                nc.sync.dma_start(
+                    out=scale_table[SCALE_ROWS * g + r : P : QUADRANT, :].bitcast(I32),
+                    in_=x_scales[g, r :: SCALE_ROWS, :].bitcast(I32),
+                )
+
         nc.vector.memset(scale_table[:].bitcast(I32), 0)
         load_w1(0)
-        for q in range(P // QUADRANT):
-            nc.sync.dma_start(
-                out=scale_table[QUADRANT * q : QUADRANT * q + SCALE_ROWS * PASSES, :].bitcast(I32),
-                in_=x_scales[:, SCALE_ROWS * q : SCALE_ROWS * (q + 1), :].bitcast(I32),
-            )
+        for r in range(0, SCALE_ROWS // 2):
+            load_scale_rows(r)
         nc.sync.dma_start(offs_sb[:], offs)
         load_w1(1)
+        for r in range(SCALE_ROWS // 2, SCALE_ROWS):
+            load_scale_rows(r)
         load_x(0)
         load_x(1)
         nc.sync.dma_start(p1_sb[:], p1)
@@ -81,9 +87,6 @@ def tile_picked_opening_none_p_kernel(tc, x_words, x_scales, w1, w2, offs, p1, p
         nc.sync.dma_start(out=w2_raw[:], in_=w2.rearrange("(p j) n -> p j n", j=PACK))
         nc.sync.dma_start(q1_sb[:], q1)
         nc.sync.dma_start(q2_sb[:], q2)
-
-        x_scale = held([P, S], U8, "x_scale")
-        nc.vector.tensor_copy(x_scale[:], scale_table[:].indirect(offs_sb[:]))
 
         w1_codes, w1_scale = {}, {}
         for g in range(PASSES):
@@ -98,6 +101,8 @@ def tile_picked_opening_none_p_kernel(tc, x_words, x_scales, w1, w2, offs, p1, p
                     w1_codes[g, PAIR * u + e] = codes[:, e * P : (e + 1) * P]
                     w1_scale[g, PAIR * u + e] = scale[:, e * P : (e + 1) * P]
 
+        x_scale = held([P, S], U8, "x_scale")
+        nc.vector.tensor_copy(x_scale[:], scale_table[:].indirect(offs_sb[:]))
         x_codes = [held([P, S], U32, "x_codes%d" % g) for g in range(PASSES)]
         nc.vector.tensor_copy(x_codes[0][:], x_table[0][:].indirect(offs_sb[:]))
 

@@ -24,12 +24,12 @@ QUADRANT = 32
 SCALE_ROWS = 4
 LIST_COLUMN = 16
 LINE = 4
-HALF = S // 2
+HALF, QUARTER = S // 2, S // 4
 Y_WINDOW = 2 * S
 CHUNKS = ((0, 256), (256, 128), (384, 128))
 LAST = len(CHUNKS) - 1
 PSUM_BANKS = 8
-CHUNK_BANKS = ((6, 7), (3,), (4, 5))
+CHUNK_BANKS = ((6, 7), (3,), (4, 5, 0, 1))
 
 
 def tile_picked_opening_none_p_kernel(tc, x_words, x_scales, w1, w2, offs, p1, p2, q1, q2, out):
@@ -55,12 +55,12 @@ def tile_picked_opening_none_p_kernel(tc, x_words, x_scales, w1, w2, offs, p1, p
         banks = [psum.tile([P, S], F32, name="bank%d" % b) for b in range(PSUM_BANKS)]
 
         w1_raw = [held([P, PACK, H], F32, "w1_raw%d" % g) for g in range(PASSES)]
-        x_table = [held([P, T], U32, "x_table%d" % g) for g in range(PASSES)]
-        scale_table = held([P, T], U8, "scale_table")
+        x_table = [shared([P, T], U32, "x_table%d" % g, "x_table%d" % g) for g in range(PASSES)]
+        scale_table = shared([P, T], U8, "scale_table", "scale_table")
         w2_raw = held([P, PACK, N], F32, "w2_raw")
 
         def load_w1(g):
-            nc.sync.dma_start(out=w1_raw[g][:], in_=w1[g * K_PASS : (g + 1) * K_PASS, :].rearrange("(p j) c -> p j c", j=PACK))
+            nc.sync.dma_start(out=w1_raw[g][:], in_=w1[g * K_PASS : (g + 1) * K_PASS, :].rearrange("(p j) n -> p j n", j=PACK))
 
         def load_x(g):
             nc.sync.dma_start(out=x_table[g][:].bitcast(I32), in_=x_words[g].rearrange("p n t -> p (n t)").bitcast(I32))
@@ -88,21 +88,31 @@ def tile_picked_opening_none_p_kernel(tc, x_words, x_scales, w1, w2, offs, p1, p
         nc.sync.dma_start(q1_sb[:], q1)
         nc.sync.dma_start(q2_sb[:], q2)
 
-        w1_codes, w1_scale = {}, {}
-        for g in range(PASSES):
+        w1_woven, w1_codes, w1_scale = {}, {}, {}
+
+        def round_w1(g, u):
             dealt = w1_raw[g][:].rearrange("p j (m t) -> p m t j", t=PACK)
-            for u, copy in enumerate((nc.vector.tensor_copy, nc.scalar.copy)):
-                w1_woven = held([P, PAIR * P * PACK], BF16, "w1_woven%d_%d" % (g, u))
-                copy(w1_woven[:].rearrange("p (t m j) -> p m t j", t=PAIR, j=PACK), dealt[:, :, PAIR * u : PAIR * (u + 1), :])
-                codes = held([P, PAIR * P], U32, "w1_codes%d_%d" % (g, u))
-                scale = held([P, PAIR * P], U8, "w1_scale%d_%d" % (g, u))
-                nc.vector.quantize_mx(out=codes[:].bitcast(FP8X4), scales=scale[:], in_=w1_woven[:])
-                for e in range(PAIR):
-                    w1_codes[g, PAIR * u + e] = codes[:, e * P : (e + 1) * P]
-                    w1_scale[g, PAIR * u + e] = scale[:, e * P : (e + 1) * P]
+            w1_woven[g, u] = held([P, PAIR * P * PACK], BF16, "w1_woven%d_%d" % (g, u))
+            copy = nc.vector.tensor_copy if g == 0 and u == 0 else nc.scalar.copy
+            copy(w1_woven[g, u][:].rearrange("p (t m j) -> p m t j", t=PAIR, j=PACK), dealt[:, :, PAIR * u : PAIR * (u + 1), :])
+
+        def quantise_w1(g, u, tag):
+            codes = shared([P, PAIR * P], U32, "w1_codes%d_%d" % (g, u), tag)
+            scale = held([P, PAIR * P], U8, "w1_scale%d_%d" % (g, u))
+            nc.vector.quantize_mx(out=codes[:].bitcast(FP8X4), scales=scale[:], in_=w1_woven[g, u][:])
+            for e in range(PAIR):
+                w1_codes[g, PAIR * u + e] = codes[:, e * P : (e + 1) * P]
+                w1_scale[g, PAIR * u + e] = scale[:, e * P : (e + 1) * P]
+
+        for g in range(PASSES):
+            for u in range(PACK // PAIR):
+                round_w1(g, u)
+        quantise_w1(0, 0, "w1_codes0_0")
+        quantise_w1(0, 1, "w1_codes0_1")
 
         x_scale = held([P, S], U8, "x_scale")
         nc.vector.tensor_copy(x_scale[:], scale_table[:].indirect(offs_sb[:]))
+        quantise_w1(1, 0, "scale_table")
         x_codes = [held([P, S], U32, "x_codes%d" % g) for g in range(PASSES)]
         nc.vector.tensor_copy(x_codes[0][:], x_table[0][:].indirect(offs_sb[:]))
 
@@ -118,29 +128,29 @@ def tile_picked_opening_none_p_kernel(tc, x_words, x_scales, w1, w2, offs, p1, p
             )
 
         pieces = [
-            (banks[0][:, 0:HALF], 0, slice(0, HALF)),
-            (banks[1][:, 0:P], 0, slice(HALF, HALF + P)),
-            (banks[5][:, 0:P], 0, slice(HALF + P, S)),
-            (banks[2][:], 1, slice(0, S)),
+            (banks[0][:, 0:HALF], slice(0, HALF)),
+            (banks[1][:, 0:QUARTER], slice(HALF, HALF + QUARTER)),
+            (banks[2][:, 0:QUARTER], slice(HALF + QUARTER, S)),
         ]
-        for acc, t, cells in pieces:
-            first_product(acc, t, 0, cells)
+        for acc, cells in pieces:
+            first_product(acc, 0, 0, cells)
         for first in (0, HALF):
             nc.vector.tensor_copy(x_codes[1][:, first : first + HALF], x_table[1][:].indirect(offs_sb[:, entries(first, HALF)]))
+        quantise_w1(1, 1, "x_table1")
         y = [held([P, Y_WINDOW], F32, "y%d" % t) for t in range(PACK)]
-        for acc, t, cells in pieces:
-            first_product(acc, t, 1, cells)
-            nc.scalar.copy(y[t][:, cells], acc)
-        for t in range(PAIR, PACK):
-            acc = banks[t - PAIR][:]
+        for acc, cells in pieces:
+            first_product(acc, 0, 1, cells)
+            nc.scalar.copy(y[0][:, cells], acc)
+        for t in range(1, PACK):
+            acc = banks[t - 1][:]
             for g in range(PASSES):
                 first_product(acc, t, g, slice(0, S))
             nc.scalar.copy(y[t][:, 0:S], acc)
 
         w2_woven = held([P, PACK * N], BF16, "w2_woven")
         nc.scalar.copy(
-            w2_woven[:].rearrange("p (c i j) -> p c j i", i=LINE, j=PACK),
-            w2_raw[:].rearrange("p j (c i) -> p c j i", i=LINE),
+            w2_woven[:].rearrange("p (n i j) -> p n j i", i=LINE, j=PACK),
+            w2_raw[:].rearrange("p j (n i) -> p n j i", i=LINE),
         )
 
         h = [held([P, S], F32, "h%d" % t) for t in range(PACK)]
@@ -169,7 +179,7 @@ def tile_picked_opening_none_p_kernel(tc, x_words, x_scales, w1, w2, offs, p1, p
         high1_tags = ("high1_0", "low0", "z0")
         high2_tags = ("high2_0", "z0", "z1")
         low, high1, high2, most, z, z_woven = [], [], [], [], [], []
-        out_view = out.rearrange("(a p) j -> p a j", p=P)
+        out_view = out.rearrange("(a p) n -> p a n", p=P)
 
         def open_low(c):
             low.append(shared([P, 2 * PAIR, CHUNKS[c][1]], BF16, "low%d" % c, low_tags[c]))
@@ -208,17 +218,17 @@ def tile_picked_opening_none_p_kernel(tc, x_words, x_scales, w1, w2, offs, p1, p
 
         def woven_max(c, u):
             nc.vector.tensor_tensor(
-                z_woven[c][:].rearrange("p (c t) -> p c t", t=PACK)[:, :, pair(u)],
-                most[c][:, pair(u), :].rearrange("p t c -> p c t"),
-                by_q2(c, u).rearrange("p t c -> p c t"),
+                z_woven[c][:].rearrange("p (n t) -> p n t", t=PACK)[:, :, pair(u)],
+                most[c][:, pair(u), :].rearrange("p t n -> p n t"),
+                by_q2(c, u).rearrange("p t n -> p n t"),
                 MAX,
             )
 
         def weave(c):
             z_woven.append(shared([P, PACK * CHUNKS[c][1]], BF16, "z_woven%d" % c, "z_woven%d" % c))
             nc.scalar.copy(
-                z_woven[c][:].rearrange("p (c i t) -> p c t i", i=LINE, t=PACK),
-                z[c][:].rearrange("p t (c i) -> p c t i", i=LINE),
+                z_woven[c][:].rearrange("p (n i t) -> p n t i", i=LINE, t=PACK),
+                z[c][:].rearrange("p t (n i) -> p n t i", i=LINE),
             )
 
         def second_product(c):
@@ -241,13 +251,13 @@ def tile_picked_opening_none_p_kernel(tc, x_words, x_scales, w1, w2, offs, p1, p
                         stop=True,
                     )
                 rows = slice(b * per_bank, (b + 1) * per_bank)
-                staged = result[:, rows, :].rearrange("p a j -> p (a j)")
-                if c == LAST and b == 1:
+                staged = result[:, rows, :].rearrange("p a n -> p (a n)")
+                if c == LAST and b % 2 == 1:
                     nc.vector.tensor_copy(staged, banks[bank][:, 0 : per_bank * width])
                 else:
                     nc.scalar.copy(staged, banks[bank][:, 0 : per_bank * width])
                 if c == LAST:
-                    queue = nc.scalar if b == 0 else nc.sync
+                    queue = nc.scalar if b == 2 else nc.sync
                     queue.dma_start(out=out_view[:, rows, first : first + width], in_=result[:, rows, :])
             if c != LAST:
                 nc.sync.dma_start(out=out_view[:, :, first : first + width], in_=result[:])

@@ -153,83 +153,86 @@ def tile_picked_opening_none_p_kernel(tc, x_words, x_scales, w1, w2, offs, p1, p
             w2_raw[:].rearrange("p j (n i) -> p n j i", i=LINE),
         )
 
-        h = [held([P, S], F32, "h%d" % t) for t in range(PACK)]
+        h = [held([P, Y_WINDOW if t < PAIR else S], F32, "h%d" % t) for t in range(PACK)]
         h_round = held([P, PACK, S], BF16, "h_round")
-        near1 = [held([P, S], F32, "near1_%d" % t) for t in range(PACK)]
-        near2 = [held([P, S], F32, "near2_%d" % t) for t in range(PACK)]
-        least = [held([P, S], F32, "least%d" % t) for t in range(PACK)]
+        near1 = [held([P, PAIR * S], F32, "near1_%d" % u) for u in range(PACK // PAIR)]
+        near2 = [held([P, PAIR * S], F32, "near2_%d" % u) for u in range(PACK // PAIR)]
+        least = [held([P, PAIR * S], F32, "least%d" % u) for u in range(PACK // PAIR)]
+
+        def plane(tile, t, width=S):
+            return tile[:, (t % PAIR) * width : (t % PAIR + 1) * width]
+
+        def erode1(t):
+            nc.vector.tensor_copy(plane(near1[t // PAIR], t), y[t][:].indirect(p1_sb[:]))
+
+        def erode2(t):
+            nc.vector.tensor_copy(plane(near2[t // PAIR], t), y[t][:].indirect(p2_sb[:]))
+
+        def first_min(u):
+            nc.vector.tensor_tensor(least[u][:], near1[u][:], near2[u][:], MIN)
 
         def second_min(t):
-            nc.vector.tensor_tensor(h[t][:], least[t][:], near2[t][:], MIN)
-            nc.scalar.copy(h_round[:, t, :], h[t][:])
+            nc.vector.tensor_tensor(h[t][:, 0:S], plane(least[t // PAIR], t), y[t][:, 0:S], MIN)
+            nc.scalar.copy(h_round[:, t, :], h[t][:, 0:S])
 
-        for t in range(PACK):
-            nc.vector.tensor_copy(near1[t][:], y[t][:].indirect(p1_sb[:]))
-            if t > 0:
-                second_min(t - 1)
-            nc.vector.tensor_copy(near2[t][:], y[t][:].indirect(p2_sb[:]))
-            nc.vector.tensor_tensor(least[t][:], near1[t][:], y[t][:, 0:S], MIN)
+        low1 = held([P, PAIR * S], BF16, "low1")
+        low2 = held([P, PAIR * S], BF16, "low2")
+        low_most = held([P, PAIR * S], BF16, "low_most")
+        low_z = held([P, PAIR * S], BF16, "low_z")
+        z_woven = [held([P, PACK * width], BF16, "z_woven%d" % c) for c, (first, width) in enumerate(CHUNKS)]
+
+        def pairs(flat):
+            return flat.rearrange("p (t n) -> p t n", t=PAIR)
+
+        def cellwise(flat):
+            return flat.rearrange("p (t n) -> p n t", t=PAIR)
+
+        def woven_pair(c, u):
+            return z_woven[c][:].rearrange("p (n t) -> p n t", t=PACK)[:, :, PAIR * u : PAIR * (u + 1)]
+
+        erode1(0)
+        erode2(0)
+        erode1(1)
+        erode2(1)
+        erode1(2)
+        first_min(0)
+        erode2(2)
+        second_min(0)
+        erode1(3)
+        second_min(1)
+        erode2(3)
+        nc.vector.tensor_copy(plane(low1, 0), h[0][:].indirect(q1_sb[:]))
+        first_min(1)
+        nc.vector.tensor_copy(plane(low2, 0), h[0][:].indirect(q2_sb[:]))
+        second_min(2)
+        nc.vector.tensor_copy(plane(low1, 1), h[1][:].indirect(q1_sb[:]))
+        second_min(3)
+        nc.vector.tensor_copy(plane(low2, 1), h[1][:].indirect(q2_sb[:]))
 
         w2_codes = held([P, N], U32, "w2_codes")
         w2_scale = held([P, N], U8, "w2_scale")
         nc.vector.quantize_mx(out=w2_codes[:].bitcast(FP8X4), scales=w2_scale[:], in_=w2_woven[:])
-        second_min(PACK - 1)
 
-        low_tags = ("low0", "high1_0", "z_woven0")
-        high1_tags = ("high1_0", "low0", "z0")
-        high2_tags = ("high2_0", "z0", "z1")
-        low, high1, high2, most, z, z_woven = [], [], [], [], [], []
+        arena = held([P, 1024], BF16, "arena")
+        high1 = [held([P, 512], BF16, "high1_0")[:], held([P, 256], BF16, "high1_1")[:], arena[:, 384:640]]
+        high2 = [held([P, 512], BF16, "high2_0")[:], arena[:, 0:256], arena[:, 640:896]]
+        most = [arena[:, 0:512], held([P, 256], BF16, "most1")[:], held([P, 256], BF16, "most2")[:]]
+        high_z = [arena[:, 512:1024], held([P, 256], BF16, "high_z1")[:]]
         out_view = out.rearrange("(a p) n -> p a n", p=P)
 
-        def open_low(c):
-            low.append(shared([P, 2 * PAIR, CHUNKS[c][1]], BF16, "low%d" % c, low_tags[c]))
-
-        def open_high1(c):
-            high1.append(shared([P, PAIR, CHUNKS[c][1]], BF16, "high1_%d" % c, high1_tags[c]))
-            most.append(held([P, PACK, CHUNKS[c][1]], BF16, "most%d" % c))
-
-        def open_high2(c):
-            high2.append(shared([P, PAIR, CHUNKS[c][1]], BF16, "high2_%d" % c, high2_tags[c]))
-
-        def open_z(c):
-            z.append(shared([P, PACK, CHUNKS[c][1]], BF16, "z%d" % c, "z%d" % c))
-
         def fetch1(c, t):
-            dst = low[c][:, t, :] if t < PAIR else high1[c][:, t - PAIR, :]
-            nc.vector.tensor_copy(dst, h[t][:].indirect(q1_sb[:, entries(*CHUNKS[c])]))
+            nc.vector.tensor_copy(plane(high1[c], t, CHUNKS[c][1]), h[t][:].indirect(q1_sb[:, entries(*CHUNKS[c])]))
 
         def fetch2(c, t):
-            dst = low[c][:, PAIR + t, :] if t < PAIR else high2[c][:, t - PAIR, :]
-            nc.vector.tensor_copy(dst, h[t][:].indirect(q2_sb[:, entries(*CHUNKS[c])]))
+            nc.vector.tensor_copy(plane(high2[c], t, CHUNKS[c][1]), h[t][:].indirect(q2_sb[:, entries(*CHUNKS[c])]))
 
-        def pair(u):
-            return slice(PAIR * u, PAIR * (u + 1))
-
-        def first_max(c, u):
+        def first_max(c):
             first, width = CHUNKS[c]
-            by_q1 = low[c][:, pair(0), :] if u == 0 else high1[c][:]
-            nc.vector.tensor_tensor(most[c][:, pair(u), :], by_q1, h_round[:, pair(u), first : first + width], MAX)
+            nc.vector.tensor_tensor(pairs(most[c]), pairs(high1[c]), h_round[:, PAIR:PACK, first : first + width], MAX)
 
-        def by_q2(c, u):
-            return low[c][:, pair(1), :] if u == 0 else high2[c][:]
-
-        def second_max(c, u):
-            nc.vector.tensor_tensor(z[c][:, pair(u), :], most[c][:, pair(u), :], by_q2(c, u), MAX)
-
-        def woven_max(c, u):
-            nc.vector.tensor_tensor(
-                z_woven[c][:].rearrange("p (n t) -> p n t", t=PACK)[:, :, pair(u)],
-                most[c][:, pair(u), :].rearrange("p t n -> p n t"),
-                by_q2(c, u).rearrange("p t n -> p n t"),
-                MAX,
-            )
-
-        def weave(c):
-            z_woven.append(shared([P, PACK * CHUNKS[c][1]], BF16, "z_woven%d" % c, "z_woven%d" % c))
-            nc.scalar.copy(
-                z_woven[c][:].rearrange("p (n i t) -> p n t i", i=LINE, t=PACK),
-                z[c][:].rearrange("p t (n i) -> p n t i", i=LINE),
-            )
+        def second_max(c):
+            nc.vector.tensor_tensor(high_z[c], most[c], high2[c], MAX)
+            nc.scalar.copy(woven_pair(c, 1), cellwise(high_z[c]))
 
         def second_product(c):
             first, width = CHUNKS[c]
@@ -256,47 +259,31 @@ def tile_picked_opening_none_p_kernel(tc, x_words, x_scales, w1, w2, offs, p1, p
                     nc.vector.tensor_copy(staged, banks[bank][:, 0 : per_bank * width])
                 else:
                     nc.scalar.copy(staged, banks[bank][:, 0 : per_bank * width])
-                if c == LAST:
-                    queue = nc.scalar if b == 2 else nc.sync
-                    queue.dma_start(out=out_view[:, rows, first : first + width], in_=result[:, rows, :])
-            if c != LAST:
-                nc.sync.dma_start(out=out_view[:, :, first : first + width], in_=result[:])
+                queue = nc.scalar if c == LAST and b == 2 else nc.sync
+                queue.dma_start(out=out_view[:, rows, first : first + width], in_=result[:, rows, :])
 
-        open_low(0)
-        open_high1(0)
-        open_high2(0)
-        open_z(0)
-        for t in range(PACK):
-            fetch1(0, t)
-        fetch2(0, 0)
-        first_max(0, 0)
-        fetch2(0, 1)
-        first_max(0, 1)
+        fetch1(0, 2)
+        nc.vector.tensor_tensor(low_most[:], low1[:], h_round[:, 0:PAIR, :].rearrange("p t n -> p (t n)"), MAX)
+        fetch1(0, 3)
+        nc.vector.tensor_tensor(low_z[:], low_most[:], low2[:], MAX)
+        for c, (first, width) in enumerate(CHUNKS):
+            nc.scalar.copy(woven_pair(c, 0), cellwise(low_z[:])[:, first : first + width, :])
         fetch2(0, 2)
-        second_max(0, 0)
+        first_max(0)
         fetch2(0, 3)
-        for c in range(1, len(CHUNKS)):
-            open_low(c)
-            fetch1(c, 0)
-            second_max(c - 1, 1)
-            weave(c - 1)
-            fetch1(c, 1)
-            fetch2(c, 0)
-            open_high1(c)
-            first_max(c, 0)
-            fetch2(c, 1)
-            fetch1(c, 2)
-            if c == LAST:
-                z_woven.append(held([P, PACK * CHUNKS[c][1]], BF16, "z_woven_last"))
-                woven_max(c, 0)
-            else:
-                open_z(c)
-                second_max(c, 0)
-            fetch1(c, 3)
-            second_product(c - 1)
-            open_high2(c)
-            first_max(c, 1)
-            fetch2(c, 2)
-            fetch2(c, 3)
-        woven_max(LAST, 1)
+        fetch1(1, 2)
+        fetch1(1, 3)
+        second_max(0)
+        first_max(1)
+        fetch2(1, 2)
+        fetch2(1, 3)
+        fetch1(2, 2)
+        second_max(1)
+        second_product(0)
+        fetch1(2, 3)
+        fetch2(2, 2)
+        first_max(2)
+        fetch2(2, 3)
+        second_product(1)
+        nc.vector.tensor_tensor(woven_pair(LAST, 1), cellwise(most[LAST]), cellwise(high2[LAST]), MAX)
         second_product(LAST)

@@ -29,7 +29,7 @@ Y_WINDOW = 2 * S
 CHUNKS = ((0, 256), (256, 128), (384, 128))
 LAST = len(CHUNKS) - 1
 PSUM_BANKS = 8
-CHUNK_BANKS = ((6, 7), (3,), (4, 5, 0, 1))
+CHUNK_BANKS = ((0, 1, 2, 3), (4, 5), (6, 7, 0, 1))
 
 
 def tile_picked_opening_none_p_kernel(tc, x_words, x_scales, w1, w2, offs, p1, p2, q1, q2, out):
@@ -59,8 +59,11 @@ def tile_picked_opening_none_p_kernel(tc, x_words, x_scales, w1, w2, offs, p1, p
         scale_table = shared([P, T], U8, "scale_table", "scale_table")
         w2_raw = held([P, PACK, N], F32, "w2_raw")
 
-        def load_w1(g):
-            nc.sync.dma_start(out=w1_raw[g][:], in_=w1[g * K_PASS : (g + 1) * K_PASS, :].rearrange("(p j) n -> p j n", j=PACK))
+        def load_w1(g, rows=slice(0, PACK)):
+            nc.sync.dma_start(
+                out=w1_raw[g][:, rows, :],
+                in_=w1[g * K_PASS : (g + 1) * K_PASS, :].rearrange("(p j) n -> p j n", j=PACK)[:, rows, :],
+            )
 
         def load_x(g):
             nc.sync.dma_start(out=x_table[g][:].bitcast(I32), in_=x_words[g].rearrange("p n t -> p (n t)").bitcast(I32))
@@ -73,11 +76,12 @@ def tile_picked_opening_none_p_kernel(tc, x_words, x_scales, w1, w2, offs, p1, p
                 )
 
         nc.vector.memset(scale_table[:].bitcast(I32), 0)
-        load_w1(0)
+        load_w1(1, slice(0, PAIR))
         for r in range(0, SCALE_ROWS // 2):
             load_scale_rows(r)
         nc.sync.dma_start(offs_sb[:], offs)
-        load_w1(1)
+        load_w1(0)
+        load_w1(1, slice(PAIR, PACK))
         for r in range(SCALE_ROWS // 2, SCALE_ROWS):
             load_scale_rows(r)
         load_x(0)
@@ -138,9 +142,9 @@ def tile_picked_opening_none_p_kernel(tc, x_words, x_scales, w1, w2, offs, p1, p
             nc.vector.tensor_copy(x_codes[1][:, first : first + HALF], x_table[1][:].indirect(offs_sb[:, entries(first, HALF)]))
         quantise_w1(1, 1, "x_table1")
         y = [held([P, Y_WINDOW], F32, "y%d" % t) for t in range(PACK)]
-        for acc, cells in pieces:
+        for (acc, cells), copy in zip(pieces, (nc.scalar.copy, nc.vector.tensor_copy, nc.scalar.copy)):
             first_product(acc, 0, 1, cells)
-            nc.scalar.copy(y[0][:, cells], acc)
+            copy(y[0][:, cells], acc)
         for t in range(1, PACK):
             acc = banks[t - 1][:]
             for g in range(PASSES):

@@ -138,6 +138,7 @@ def tile_picked_opening_none_p_kernel(tc, x_words, x_scales, w1, w2, offs, p1, p
         ]
         for acc, cells in pieces:
             first_product(acc, 0, 0, cells)
+        first_product(banks[3][:], 1, 0, slice(0, S))
         for first in (0, HALF):
             nc.vector.tensor_copy(x_codes[1][:, first : first + HALF], x_table[1][:].indirect(offs_sb[:, entries(first, HALF)]))
         quantise_w1(1, 1, "x_table1")
@@ -145,7 +146,9 @@ def tile_picked_opening_none_p_kernel(tc, x_words, x_scales, w1, w2, offs, p1, p
         for (acc, cells), copy in zip(pieces, (nc.scalar.copy, nc.vector.tensor_copy, nc.scalar.copy)):
             first_product(acc, 0, 1, cells)
             copy(y[0][:, cells], acc)
-        for t in range(1, PACK):
+        first_product(banks[3][:], 1, 1, slice(0, S))
+        nc.scalar.copy(y[1][:, 0:S], banks[3][:])
+        for t in range(2, PACK):
             acc = banks[t - 1][:]
             for g in range(PASSES):
                 first_product(acc, t, g, slice(0, S))
@@ -213,13 +216,10 @@ def tile_picked_opening_none_p_kernel(tc, x_words, x_scales, w1, w2, offs, p1, p
         second_min(3)
         nc.vector.tensor_copy(plane(low2, 1), h[1][:].indirect(q2_sb[:]))
 
-        w2_codes = held([P, N], U32, "w2_codes")
-        w2_scale = held([P, N], U8, "w2_scale")
-        nc.vector.quantize_mx(out=w2_codes[:].bitcast(FP8X4), scales=w2_scale[:], in_=w2_woven[:])
 
         arena = held([P, 1024], BF16, "arena")
-        high1 = [held([P, 512], BF16, "high1_0")[:], held([P, 256], BF16, "high1_1")[:], arena[:, 384:640]]
-        high2 = [held([P, 512], BF16, "high2_0")[:], arena[:, 0:256], arena[:, 640:896]]
+        high1 = [held([P, 512], BF16, "high1_0")[:], held([P, 256], BF16, "high1_1")[:], arena[:, 512:768]]
+        high2 = [shared([P, 512], BF16, "high2_0", "high2_0")[:], arena[:, 0:256], arena[:, 768:1024]]
         most = [arena[:, 0:512], held([P, 256], BF16, "most1")[:], held([P, 256], BF16, "most2")[:]]
         high_z = [arena[:, 512:1024], held([P, 256], BF16, "high_z1")[:]]
         out_view = out.rearrange("(a p) n -> p a n", p=P)
@@ -281,13 +281,16 @@ def tile_picked_opening_none_p_kernel(tc, x_words, x_scales, w1, w2, offs, p1, p
         first_max(1)
         fetch2(1, 2)
         fetch2(1, 3)
-        fetch1(2, 2)
+        w2_codes = shared([P, N], U32, "w2_codes", "high2_0")
+        w2_scale = held([P, N], U8, "w2_scale")
+        nc.vector.quantize_mx(out=w2_codes[:].bitcast(FP8X4), scales=w2_scale[:], in_=w2_woven[:])
         second_max(1)
         second_product(0)
+        fetch1(2, 2)
         fetch1(2, 3)
-        fetch2(2, 2)
-        first_max(2)
-        fetch2(2, 3)
         second_product(1)
+        first_max(2)
+        fetch2(2, 2)
+        fetch2(2, 3)
         nc.vector.tensor_tensor(woven_pair(LAST, 1), cellwise(most[LAST]), cellwise(high2[LAST]), MAX)
         second_product(LAST)

@@ -25,8 +25,8 @@ SCALE_ROWS = 4
 LIST_COLUMN = 16
 LINE = 4
 HALF, QUARTER = S // 2, S // 4
-Y_WINDOW = 2 * S
-CHUNKS = ((0, 256), (256, 128), (384, 128))
+WIDE_WINDOW = 2 * S
+CHUNKS = ((0, HALF), (HALF, QUARTER), (HALF + QUARTER, QUARTER))
 LAST = len(CHUNKS) - 1
 PSUM_BANKS = 8
 CHUNK_BANKS = ((0, 1, 2, 3), (4, 5), (6, 7, 0, 1))
@@ -76,12 +76,12 @@ def tile_picked_opening_none_p_kernel(tc, x_words, x_scales, w1, w2, offs, p1, p
                 )
 
         nc.vector.memset(scale_table[:].bitcast(I32), 0)
-        load_w1(1, slice(0, PAIR))
+        load_w1(0, slice(0, PAIR))
         for r in range(0, SCALE_ROWS // 2):
             load_scale_rows(r)
         nc.sync.dma_start(offs_sb[:], offs)
-        load_w1(0)
-        load_w1(1, slice(PAIR, PACK))
+        load_w1(0, slice(PAIR, PACK))
+        load_w1(1)
         for r in range(SCALE_ROWS // 2, SCALE_ROWS):
             load_scale_rows(r)
         load_x(0)
@@ -97,7 +97,7 @@ def tile_picked_opening_none_p_kernel(tc, x_words, x_scales, w1, w2, offs, p1, p
         def round_w1(g, u):
             dealt = w1_raw[g][:].rearrange("p j (m t) -> p m t j", t=PACK)
             w1_woven[g, u] = held([P, PAIR * P * PACK], BF16, "w1_woven%d_%d" % (g, u))
-            copy = nc.vector.tensor_copy if g == 0 and u == 0 else nc.scalar.copy
+            copy = nc.vector.tensor_copy if g == 0 else nc.scalar.copy
             copy(w1_woven[g, u][:].rearrange("p (t m j) -> p m t j", t=PAIR, j=PACK), dealt[:, :, PAIR * u : PAIR * (u + 1), :])
 
         def quantise_w1(g, u, tag):
@@ -138,17 +138,18 @@ def tile_picked_opening_none_p_kernel(tc, x_words, x_scales, w1, w2, offs, p1, p
         ]
         for acc, cells in pieces:
             first_product(acc, 0, 0, cells)
-        first_product(banks[3][:], 1, 0, slice(0, S))
+        plane1_bank = banks[len(pieces)]
+        first_product(plane1_bank[:], 1, 0, slice(0, S))
         for first in (0, HALF):
             nc.vector.tensor_copy(x_codes[1][:, first : first + HALF], x_table[1][:].indirect(offs_sb[:, entries(first, HALF)]))
         quantise_w1(1, 1, "x_table1")
-        y = [held([P, Y_WINDOW], F32, "y%d" % t) for t in range(PACK)]
+        y = [held([P, WIDE_WINDOW], F32, "y%d" % t) for t in range(PACK)]
         for (acc, cells), copy in zip(pieces, (nc.scalar.copy, nc.vector.tensor_copy, nc.scalar.copy)):
             first_product(acc, 0, 1, cells)
             copy(y[0][:, cells], acc)
-        first_product(banks[3][:], 1, 1, slice(0, S))
-        nc.scalar.copy(y[1][:, 0:S], banks[3][:])
-        for t in range(2, PACK):
+        first_product(plane1_bank[:], 1, 1, slice(0, S))
+        nc.scalar.copy(y[1][:, 0:S], plane1_bank[:])
+        for t in range(PAIR, PACK):
             acc = banks[t - 1][:]
             for g in range(PASSES):
                 first_product(acc, t, g, slice(0, S))
@@ -160,7 +161,7 @@ def tile_picked_opening_none_p_kernel(tc, x_words, x_scales, w1, w2, offs, p1, p
             w2_raw[:].rearrange("p j (n i) -> p n j i", i=LINE),
         )
 
-        h = [held([P, Y_WINDOW if t < PAIR else S], F32, "h%d" % t) for t in range(PACK)]
+        h = [held([P, WIDE_WINDOW if t < PAIR else S], F32, "h%d" % t) for t in range(PACK)]
         h_round = held([P, PACK, S], BF16, "h_round")
         near1 = [held([P, PAIR * S], F32, "near1_%d" % u) for u in range(PACK // PAIR)]
         near2 = [held([P, PAIR * S], F32, "near2_%d" % u) for u in range(PACK // PAIR)]
@@ -188,6 +189,9 @@ def tile_picked_opening_none_p_kernel(tc, x_words, x_scales, w1, w2, offs, p1, p
         low_z = held([P, PAIR * S], BF16, "low_z")
         z_woven = [held([P, PACK * width], BF16, "z_woven%d" % c) for c, (first, width) in enumerate(CHUNKS)]
 
+        def dilate_low(dst, t, offsets):
+            nc.vector.tensor_copy(plane(dst, t), h[t][:].indirect(offsets[:]))
+
         def pairs(flat):
             return flat.rearrange("p (t n) -> p t n", t=PAIR)
 
@@ -208,20 +212,21 @@ def tile_picked_opening_none_p_kernel(tc, x_words, x_scales, w1, w2, offs, p1, p
         erode1(3)
         second_min(1)
         erode2(3)
-        nc.vector.tensor_copy(plane(low1, 0), h[0][:].indirect(q1_sb[:]))
+        dilate_low(low1, 0, q1_sb)
         first_min(1)
-        nc.vector.tensor_copy(plane(low2, 0), h[0][:].indirect(q2_sb[:]))
+        dilate_low(low2, 0, q2_sb)
         second_min(2)
-        nc.vector.tensor_copy(plane(low1, 1), h[1][:].indirect(q1_sb[:]))
+        dilate_low(low1, 1, q1_sb)
         second_min(3)
-        nc.vector.tensor_copy(plane(low2, 1), h[1][:].indirect(q2_sb[:]))
+        dilate_low(low2, 1, q2_sb)
 
-
-        arena = held([P, 1024], BF16, "arena")
-        high1 = [held([P, 512], BF16, "high1_0")[:], held([P, 256], BF16, "high1_1")[:], arena[:, 512:768]]
-        high2 = [shared([P, 512], BF16, "high2_0", "high2_0")[:], arena[:, 0:256], arena[:, 768:1024]]
-        most = [arena[:, 0:512], held([P, 256], BF16, "most1")[:], held([P, 256], BF16, "most2")[:]]
-        high_z = [arena[:, 512:1024], held([P, 256], BF16, "high_z1")[:]]
+        wide, narrow = PAIR * HALF, PAIR * QUARTER
+        reused = held([P, 2 * wide], BF16, "reused")
+        most0, high_z0 = reused[:, 0:wide], reused[:, wide : 2 * wide]
+        high1 = [held([P, wide], BF16, "high1_0")[:], held([P, narrow], BF16, "high1_1")[:], high_z0[:, 0:narrow]]
+        high2 = [shared([P, wide], BF16, "high2_0", "high2_0")[:], most0[:, 0:narrow], high_z0[:, narrow:wide]]
+        most = [most0, held([P, narrow], BF16, "most1")[:], held([P, narrow], BF16, "most2")[:]]
+        high_z = [high_z0, held([P, narrow], BF16, "high_z1")[:]]
         out_view = out.rearrange("(a p) n -> p a n", p=P)
 
         def fetch1(c, t):
@@ -263,7 +268,7 @@ def tile_picked_opening_none_p_kernel(tc, x_words, x_scales, w1, w2, offs, p1, p
                     nc.vector.tensor_copy(staged, banks[bank][:, 0 : per_bank * width])
                 else:
                     nc.scalar.copy(staged, banks[bank][:, 0 : per_bank * width])
-                queue = nc.scalar if c == LAST and b == 2 else nc.sync
+                queue = nc.scalar if c == LAST and b == len(CHUNK_BANKS[c]) - 2 else nc.sync
                 queue.dma_start(out=out_view[:, rows, first : first + width], in_=result[:, rows, :])
 
         fetch1(0, 2)

@@ -77,10 +77,10 @@ def tile_picked_opening_none_p_kernel(tc, x_words, x_scales, w1, w2, offs, p1, p
 
         nc.vector.memset(scale_table[:].bitcast(I32), 0)
         load_w1(0, slice(0, PAIR))
+        load_w1(0, slice(PAIR, PACK))
         for r in range(0, SCALE_ROWS // 2):
             load_scale_rows(r)
         nc.sync.dma_start(offs_sb[:], offs)
-        load_w1(0, slice(PAIR, PACK))
         load_w1(1)
         for r in range(SCALE_ROWS // 2, SCALE_ROWS):
             load_scale_rows(r)

@@ -118,7 +118,8 @@ def tile_picked_opening_none_p_kernel(tc, x_words, x_scales, w1, w2, offs, p1, p
         nc.vector.tensor_copy(x_scale[:], scale_table[:].indirect(offs_sb[:]))
         quantise_w1(1, 0, "scale_table")
         x_codes = [held([P, S], U32, "x_codes%d" % g) for g in range(PASSES)]
-        nc.vector.tensor_copy(x_codes[0][:], x_table[0][:].indirect(offs_sb[:]))
+        for first in (0, HALF):
+            nc.vector.tensor_copy(x_codes[0][:, first : first + HALF], x_table[0][:].indirect(offs_sb[:, entries(first, HALF)]))
 
         def first_product(acc, t, g, cells):
             nc.tensor.matmul_mx(
@@ -140,6 +141,8 @@ def tile_picked_opening_none_p_kernel(tc, x_words, x_scales, w1, w2, offs, p1, p
             first_product(acc, 0, 0, cells)
         plane1_bank = banks[len(pieces)]
         first_product(plane1_bank[:], 1, 0, slice(0, S))
+        plane2_bank = banks[len(pieces) + 1]
+        first_product(plane2_bank[:], 2, 0, slice(0, S))
         for first in (0, HALF):
             nc.vector.tensor_copy(x_codes[1][:, first : first + HALF], x_table[1][:].indirect(offs_sb[:, entries(first, HALF)]))
         quantise_w1(1, 1, "x_table1")
@@ -149,11 +152,11 @@ def tile_picked_opening_none_p_kernel(tc, x_words, x_scales, w1, w2, offs, p1, p
             copy(y[0][:, cells], acc)
         first_product(plane1_bank[:], 1, 1, slice(0, S))
         nc.scalar.copy(y[1][:, 0:S], plane1_bank[:])
-        for t in range(PAIR, PACK):
-            acc = banks[t - 1][:]
-            for g in range(PASSES):
-                first_product(acc, t, g, slice(0, S))
-            nc.scalar.copy(y[t][:, 0:S], acc)
+        first_product(plane2_bank[:], 2, 1, slice(0, S))
+        nc.scalar.copy(y[2][:, 0:S], plane2_bank[:])
+        for g in range(PASSES):
+            first_product(banks[1][:], 3, g, slice(0, S))
+        nc.scalar.copy(y[3][:, 0:S], banks[1][:])
 
         w2_woven = held([P, PACK * N], BF16, "w2_woven")
         nc.scalar.copy(
@@ -247,7 +250,13 @@ def tile_picked_opening_none_p_kernel(tc, x_words, x_scales, w1, w2, offs, p1, p
             first, width = CHUNKS[c]
             z_codes = held([P, width], U32, "z_codes%d" % c)
             z_scale = held([P, width], U8, "z_scale%d" % c)
-            nc.vector.quantize_mx(out=z_codes[:].bitcast(FP8X4), scales=z_scale[:], in_=z_woven[c][:])
+            step = width // 2 if c == LAST else width
+            for n in range(0, width, step):
+                nc.vector.quantize_mx(
+                    out=z_codes[:, n : n + step].bitcast(FP8X4),
+                    scales=z_scale[:, n : n + step],
+                    in_=z_woven[c][:, PACK * n : PACK * (n + step)],
+                )
             result = held([P, N // P, width], F32, "result%d" % c)
             per_bank = (N // P) // len(CHUNK_BANKS[c])
             for b, bank in enumerate(CHUNK_BANKS[c]):
@@ -297,5 +306,7 @@ def tile_picked_opening_none_p_kernel(tc, x_words, x_scales, w1, w2, offs, p1, p
         first_max(2)
         fetch2(2, 2)
         fetch2(2, 3)
-        nc.vector.tensor_tensor(woven_pair(LAST, 1), cellwise(most[LAST]), cellwise(high2[LAST]), MAX)
+        for n in (0, QUARTER // 2):
+            cells = slice(n, n + QUARTER // 2)
+            nc.vector.tensor_tensor(woven_pair(LAST, 1)[:, cells, :], cellwise(most[LAST])[:, cells, :], cellwise(high2[LAST])[:, cells, :], MAX)
         second_product(LAST)

@@ -97,7 +97,7 @@ def tile_picked_opening_none_p_kernel(tc, x_words, x_scales, w1, w2, offs, p1, p
         def round_w1(g, u):
             dealt = w1_raw[g][:].rearrange("p j (m t) -> p m t j", t=PACK)
             w1_woven[g, u] = held([P, PAIR * P * PACK], BF16, "w1_woven%d_%d" % (g, u))
-            copy = nc.vector.tensor_copy if g == 0 else nc.scalar.copy
+            copy = nc.scalar.copy if (g, u) == (1, 0) else nc.vector.tensor_copy
             copy(w1_woven[g, u][:].rearrange("p (t m j) -> p m t j", t=PAIR, j=PACK), dealt[:, :, PAIR * u : PAIR * (u + 1), :])
 
         def quantise_w1(g, u, tag):
@@ -158,7 +158,7 @@ def tile_picked_opening_none_p_kernel(tc, x_words, x_scales, w1, w2, offs, p1, p
             first_product(banks[1][:], 3, g, slice(0, S))
         nc.scalar.copy(y[3][:, 0:S], banks[1][:])
 
-        w2_woven = held([P, PACK * N], BF16, "w2_woven")
+        w2_woven = shared([P, PACK * N], BF16, "w2_woven", "x_table1")
         nc.scalar.copy(
             w2_woven[:].rearrange("p (n i j) -> p n j i", i=LINE, j=PACK),
             w2_raw[:].rearrange("p j (n i) -> p n j i", i=LINE),
@@ -280,12 +280,12 @@ def tile_picked_opening_none_p_kernel(tc, x_words, x_scales, w1, w2, offs, p1, p
                 queue = nc.scalar if c == LAST and b == len(CHUNK_BANKS[c]) - 2 else nc.sync
                 queue.dma_start(out=out_view[:, rows, first : first + width], in_=result[:, rows, :])
 
-        fetch1(0, 2)
         nc.vector.tensor_tensor(low_most[:], low1[:], h_round[:, 0:PAIR, :].rearrange("p t n -> p (t n)"), MAX)
-        fetch1(0, 3)
+        fetch1(0, 2)
         nc.vector.tensor_tensor(low_z[:], low_most[:], low2[:], MAX)
         for c, (first, width) in enumerate(CHUNKS):
             nc.scalar.copy(woven_pair(c, 0), cellwise(low_z[:])[:, first : first + width, :])
+        fetch1(0, 3)
         fetch2(0, 2)
         first_max(0)
         fetch2(0, 3)

@@ -14,6 +14,7 @@ U8 = mybir.dt.uint8
 FP8X4 = mybir.dt.float8_e4m3fn_x4
 MIN = mybir.AluOpType.min
 MAX = mybir.AluOpType.max
+COPY = mybir.ActivationFunctionType.Copy
 
 P = 128
 PACK = 4
@@ -151,112 +152,79 @@ def tile_picked_opening_none_p_kernel(tc, x_words, x_scales, w1, w2, offs, p1, p
             first_product(acc, 0, 1, cells)
             copy(y[0][:, cells], acc)
         first_product(plane1_bank[:], 1, 1, slice(0, S))
-        nc.scalar.copy(y[1][:, 0:S], plane1_bank[:])
         first_product(plane2_bank[:], 2, 1, slice(0, S))
-        nc.scalar.copy(y[2][:, 0:S], plane2_bank[:])
         for g in range(PASSES):
             first_product(banks[1][:], 3, g, slice(0, S))
-        nc.scalar.copy(y[3][:, 0:S], banks[1][:])
 
-        w2_woven = shared([P, PACK * N], BF16, "w2_woven", "x_table1")
-        nc.scalar.copy(
-            w2_woven[:].rearrange("p (n i j) -> p n j i", i=LINE, j=PACK),
-            w2_raw[:].rearrange("p j (n i) -> p n j i", i=LINE),
-        )
+
+        y_bank = {1: plane1_bank, 2: plane2_bank, 3: banks[1]}
+
+        def leave_psum(t):
+            nc.scalar.copy(y[t][:, 0:S], y_bank[t][:])
+
+        def gather(engine, dst, window, offsets):
+            if engine == "scalar":
+                nc.scalar.activation(dst, window.indirect(offsets), COPY)
+            else:
+                nc.vector.tensor_copy(dst, window.indirect(offsets))
 
         h = [held([P, WIDE_WINDOW if t < PAIR else S], F32, "h%d" % t) for t in range(PACK)]
-        h_round = held([P, PACK, S], BF16, "h_round")
-        near1 = [held([P, PAIR * S], F32, "near1_%d" % u) for u in range(PACK // PAIR)]
-        near2 = [held([P, PAIR * S], F32, "near2_%d" % u) for u in range(PACK // PAIR)]
-        least = [held([P, PAIR * S], F32, "least%d" % u) for u in range(PACK // PAIR)]
+        near1 = [held([P, S], F32, "near1_%d" % t) for t in range(PACK)]
+        near2 = [held([P, S], F32, "near2_%d" % t) for t in range(PACK)]
+        least = [held([P, S], F32, "least%d" % t) for t in range(PACK)]
 
-        def plane(tile, t, width=S):
-            return tile[:, (t % PAIR) * width : (t % PAIR + 1) * width]
+        def erode1(t, engine):
+            gather(engine, near1[t][:], y[t][:], p1_sb[:])
 
-        def erode1(t):
-            nc.vector.tensor_copy(plane(near1[t // PAIR], t), y[t][:].indirect(p1_sb[:]))
+        def erode2(t, engine):
+            gather(engine, near2[t][:], y[t][:], p2_sb[:])
 
-        def erode2(t):
-            nc.vector.tensor_copy(plane(near2[t // PAIR], t), y[t][:].indirect(p2_sb[:]))
-
-        def first_min(u):
-            nc.vector.tensor_tensor(least[u][:], near1[u][:], near2[u][:], MIN)
+        def first_min(t):
+            nc.vector.tensor_tensor(least[t][:], near1[t][:], y[t][:, 0:S], MIN)
 
         def second_min(t):
-            nc.vector.tensor_tensor(h[t][:, 0:S], plane(least[t // PAIR], t), y[t][:, 0:S], MIN)
-            nc.scalar.copy(h_round[:, t, :], h[t][:, 0:S])
+            nc.vector.tensor_tensor(h[t][:, 0:S], least[t][:], near2[t][:], MIN)
 
-        low1 = held([P, PAIR * S], BF16, "low1")
-        low2 = held([P, PAIR * S], BF16, "low2")
-        low_most = held([P, PAIR * S], BF16, "low_most")
-        low_z = held([P, PAIR * S], BF16, "low_z")
+        w2_woven = held([P, PACK * N], BF16, "w2_woven")
+        w2_codes = held([P, N], U32, "w2_codes")
+        w2_scale = held([P, N], U8, "w2_scale")
+
+        far1 = [held([P, S], BF16, "far1_%d" % t) for t in range(PACK)]
+        far2 = held([P, PACK * S], BF16, "far2")
+        most = held([P, PACK * S], BF16, "most")
         z_woven = [held([P, PACK * width], BF16, "z_woven%d" % c) for c, (first, width) in enumerate(CHUNKS)]
-
-        def dilate_low(dst, t, offsets):
-            nc.vector.tensor_copy(plane(dst, t), h[t][:].indirect(offsets[:]))
-
-        def pairs(flat):
-            return flat.rearrange("p (t n) -> p t n", t=PAIR)
-
-        def cellwise(flat):
-            return flat.rearrange("p (t n) -> p n t", t=PAIR)
-
-        def woven_pair(c, u):
-            return z_woven[c][:].rearrange("p (n t) -> p n t", t=PACK)[:, :, PAIR * u : PAIR * (u + 1)]
-
-        erode1(0)
-        erode2(0)
-        erode1(1)
-        erode2(1)
-        erode1(2)
-        first_min(0)
-        erode2(2)
-        second_min(0)
-        erode1(3)
-        second_min(1)
-        erode2(3)
-        dilate_low(low1, 0, q1_sb)
-        first_min(1)
-        dilate_low(low2, 0, q2_sb)
-        second_min(2)
-        dilate_low(low1, 1, q1_sb)
-        second_min(3)
-        dilate_low(low2, 1, q2_sb)
-
-        wide, narrow = PAIR * HALF, PAIR * QUARTER
-        reused = held([P, 2 * wide], BF16, "reused")
-        most0, high_z0 = reused[:, 0:wide], reused[:, wide : 2 * wide]
-        high1 = [held([P, wide], BF16, "high1_0")[:], held([P, narrow], BF16, "high1_1")[:], high_z0[:, 0:narrow]]
-        high2 = [shared([P, wide], BF16, "high2_0", "high2_0")[:], most0[:, 0:narrow], high_z0[:, narrow:wide]]
-        most = [most0, held([P, narrow], BF16, "most1")[:], held([P, narrow], BF16, "most2")[:]]
-        high_z = [high_z0, held([P, narrow], BF16, "high_z1")[:]]
         out_view = out.rearrange("(a p) n -> p a n", p=P)
+        WHOLE = (0, S)
 
-        def fetch1(c, t):
-            nc.vector.tensor_copy(plane(high1[c], t, CHUNKS[c][1]), h[t][:].indirect(q1_sb[:, entries(*CHUNKS[c])]))
+        def dilate1(t, cells, engine):
+            first, width = cells
+            gather(engine, far1[t][:, first : first + width], h[t][:], q1_sb[:, entries(first, width)])
 
-        def fetch2(c, t):
-            nc.vector.tensor_copy(plane(high2[c], t, CHUNKS[c][1]), h[t][:].indirect(q2_sb[:, entries(*CHUNKS[c])]))
+        def dilate2(t, cells, engine):
+            first, width = cells
+            gather(engine, far2[:, t * S + first : t * S + first + width], h[t][:], q2_sb[:, entries(first, width)])
 
-        def first_max(c):
-            first, width = CHUNKS[c]
-            nc.vector.tensor_tensor(pairs(most[c]), pairs(high1[c]), h_round[:, PAIR:PACK, first : first + width], MAX)
+        def first_max(t, cells):
+            first, width = cells
+            nc.vector.tensor_tensor(most[:, t * S + first : t * S + first + width], far1[t][:, first : first + width], h[t][:, first : first + width], MAX)
+
+        def by_lines(flat, first, width):
+            return flat[:].rearrange("p (t n i) -> p n t i", t=PACK, i=LINE)[:, first // LINE : (first + width) // LINE, :, :]
 
         def second_max(c):
-            nc.vector.tensor_tensor(high_z[c], most[c], high2[c], MAX)
-            nc.scalar.copy(woven_pair(c, 1), cellwise(high_z[c]))
+            first, width = CHUNKS[c]
+            nc.vector.tensor_tensor(
+                z_woven[c][:].rearrange("p (n i t) -> p n t i", i=LINE, t=PACK), by_lines(most, first, width), by_lines(far2, first, width), MAX
+            )
+
+        z_codes = [held([P, width], U32, "z_codes%d" % c) for c, (first, width) in enumerate(CHUNKS)]
+        z_scale = [held([P, width], U8, "z_scale%d" % c) for c, (first, width) in enumerate(CHUNKS)]
+
+        def quantise_z(c):
+            nc.vector.quantize_mx(out=z_codes[c][:].bitcast(FP8X4), scales=z_scale[c][:], in_=z_woven[c][:])
 
         def second_product(c):
             first, width = CHUNKS[c]
-            z_codes = held([P, width], U32, "z_codes%d" % c)
-            z_scale = held([P, width], U8, "z_scale%d" % c)
-            step = width // 2 if c == LAST else width
-            for n in range(0, width, step):
-                nc.vector.quantize_mx(
-                    out=z_codes[:, n : n + step].bitcast(FP8X4),
-                    scales=z_scale[:, n : n + step],
-                    in_=z_woven[c][:, PACK * n : PACK * (n + step)],
-                )
             result = held([P, N // P, width], F32, "result%d" % c)
             per_bank = (N // P) // len(CHUNK_BANKS[c])
             for b, bank in enumerate(CHUNK_BANKS[c]):
@@ -266,8 +234,8 @@ def tile_picked_opening_none_p_kernel(tc, x_words, x_scales, w1, w2, offs, p1, p
                         out=banks[bank][:, a * width : (a + 1) * width],
                         lhsT=w2_codes[:, m * P : (m + 1) * P].bitcast(FP8X4),
                         lhsT_scale=w2_scale[:, m * P : (m + 1) * P],
-                        rhs=z_codes[:].bitcast(FP8X4),
-                        rhs_scale=z_scale[:],
+                        rhs=z_codes[c][:].bitcast(FP8X4),
+                        rhs_scale=z_scale[c][:],
                         start=True,
                         stop=True,
                     )
@@ -280,33 +248,61 @@ def tile_picked_opening_none_p_kernel(tc, x_words, x_scales, w1, w2, offs, p1, p
                 queue = nc.scalar if c == LAST and b == len(CHUNK_BANKS[c]) - 2 else nc.sync
                 queue.dma_start(out=out_view[:, rows, first : first + width], in_=result[:, rows, :])
 
-        nc.vector.tensor_tensor(low_most[:], low1[:], h_round[:, 0:PAIR, :].rearrange("p t n -> p (t n)"), MAX)
-        fetch1(0, 2)
-        nc.vector.tensor_tensor(low_z[:], low_most[:], low2[:], MAX)
-        for c, (first, width) in enumerate(CHUNKS):
-            nc.scalar.copy(woven_pair(c, 0), cellwise(low_z[:])[:, first : first + width, :])
-        fetch1(0, 3)
-        fetch2(0, 2)
-        first_max(0)
-        fetch2(0, 3)
-        fetch1(1, 2)
-        fetch1(1, 3)
-        second_max(0)
-        first_max(1)
-        fetch2(1, 2)
-        fetch2(1, 3)
-        w2_codes = shared([P, N], U32, "w2_codes", "high2_0")
-        w2_scale = held([P, N], U8, "w2_scale")
+        erode1(0, "vector")
+        leave_psum(1)
+        erode2(0, "scalar")
+        erode1(1, "vector")
+        leave_psum(2)
+        first_min(0)
+        erode2(1, "scalar")
+        nc.vector.tensor_copy(
+            w2_woven[:].rearrange("p (n i j) -> p n j i", i=LINE, j=PACK),
+            w2_raw[:].rearrange("p j (n i) -> p n j i", i=LINE),
+        )
+        leave_psum(3)
+        second_min(0)
+        first_min(1)
+        erode1(2, "scalar")
+        erode1(3, "vector")
+        second_min(1)
+        erode2(2, "scalar")
+        first_min(2)
+        erode2(3, "scalar")
+        first_min(3)
+        second_min(2)
         nc.vector.quantize_mx(out=w2_codes[:].bitcast(FP8X4), scales=w2_scale[:], in_=w2_woven[:])
+        second_min(3)
+
+        dilate1(0, WHOLE, "scalar")
+        dilate1(1, WHOLE, "scalar")
+        dilate2(0, WHOLE, "scalar")
+        dilate2(1, WHOLE, "scalar")
+        dilate1(2, CHUNKS[0], "vector")
+        first_max(0, WHOLE)
+        dilate1(3, CHUNKS[0], "vector")
+        first_max(2, CHUNKS[0])
+        first_max(1, WHOLE)
+        first_max(3, CHUNKS[0])
+        dilate2(2, CHUNKS[0], "scalar")
+        dilate2(3, CHUNKS[0], "scalar")
+        dilate1(3, CHUNKS[1], "vector")
+        dilate1(3, CHUNKS[2], "vector")
+        second_max(0)
+        dilate1(2, CHUNKS[1], "scalar")
+        dilate2(2, CHUNKS[1], "scalar")
+        dilate2(3, CHUNKS[1], "scalar")
+        first_max(3, CHUNKS[1])
+        quantise_z(0)
+        first_max(2, CHUNKS[1])
+        first_max(3, CHUNKS[2])
+        dilate1(2, CHUNKS[2], "scalar")
         second_max(1)
         second_product(0)
-        fetch1(2, 2)
-        fetch1(2, 3)
+        dilate2(2, CHUNKS[2], "scalar")
+        dilate2(3, CHUNKS[2], "scalar")
+        first_max(2, CHUNKS[2])
+        quantise_z(1)
+        second_max(2)
         second_product(1)
-        first_max(2)
-        fetch2(2, 2)
-        fetch2(2, 3)
-        for n in (0, QUARTER // 2):
-            cells = slice(n, n + QUARTER // 2)
-            nc.vector.tensor_tensor(woven_pair(LAST, 1)[:, cells, :], cellwise(most[LAST])[:, cells, :], cellwise(high2[LAST])[:, cells, :], MAX)
-        second_product(LAST)
+        quantise_z(2)
+        second_product(2)

@@ -168,9 +168,10 @@ def tile_picked_opening_none_p_kernel(tc, x_words, x_scales, w1, w2, offs, p1, p
             else:
                 nc.vector.tensor_copy(dst, window.indirect(offsets))
 
-        h = [held([P, WIDE_WINDOW if t < PAIR else S], F32, "h%d" % t) for t in range(PACK)]
+        h = [held([P, S], F32, "h%d" % t) for t in range(PACK)]
+        h_all = held([P, PACK * S], F32, "h_all")
         near1 = [held([P, S], F32, "near1_%d" % t) for t in range(PACK)]
-        near2 = [held([P, S], F32, "near2_%d" % t) for t in range(PACK)]
+        near2 = [shared([P, S], F32, "near2_%d" % t, "near2_%d" % t) for t in range(PACK)]
         least = [held([P, S], F32, "least%d" % t) for t in range(PACK)]
 
         def erode1(t, engine):
@@ -184,37 +185,49 @@ def tile_picked_opening_none_p_kernel(tc, x_words, x_scales, w1, w2, offs, p1, p
 
         def second_min(t):
             nc.vector.tensor_tensor(h[t][:, 0:S], least[t][:], near2[t][:], MIN)
+            nc.sync.dma_start(out=h_all[:, t * S : (t + 1) * S], in_=h[t][:, 0:S])
 
-        w2_woven = held([P, PACK * N], BF16, "w2_woven")
+
+        w2_woven = {}
         w2_codes = held([P, N], U32, "w2_codes")
         w2_scale = held([P, N], U8, "w2_scale")
 
-        far1 = [held([P, S], BF16, "far1_%d" % t) for t in range(PACK)]
-        far2 = held([P, PACK * S], BF16, "far2")
-        most = held([P, PACK * S], BF16, "most")
-        z_woven = [held([P, PACK * width], BF16, "z_woven%d" % c) for c, (first, width) in enumerate(CHUNKS)]
+        def weave_w2(u, tag):
+            w2_woven[u] = shared([P, PACK * N // 2], BF16, "w2_woven%d" % u, tag)
+            nc.vector.tensor_copy(
+                w2_woven[u][:].rearrange("p (n i j) -> p n j i", i=LINE, j=PACK),
+                w2_raw[:, :, u * (N // 2) : (u + 1) * (N // 2)].rearrange("p j (n i) -> p n j i", i=LINE),
+            )
+
+        def quantise_w2(u):
+            columns = slice(u * (N // 2), (u + 1) * (N // 2))
+            nc.vector.quantize_mx(out=w2_codes[:, columns].bitcast(FP8X4), scales=w2_scale[:, columns], in_=w2_woven[u][:])
+
+        far1 = [held([P, PACK * HALF], BF16, "far1_%d" % u) for u in range(2)]
+        far2 = [held([P, PACK * HALF], BF16, "far2_%d" % u) for u in range(2)]
+        z_woven = [shared([P, PACK * width], BF16, "z_woven%d" % c, "z_woven%d" % c) for c, (first, width) in enumerate(CHUNKS)]
         out_view = out.rearrange("(a p) n -> p a n", p=P)
-        WHOLE = (0, S)
 
-        def dilate1(t, cells, engine):
+        def dilate(dst, t, cells, offsets, engine):
             first, width = cells
-            gather(engine, far1[t][:, first : first + width], h[t][:], q1_sb[:, entries(first, width)])
+            at = t * HALF + first % HALF
+            gather(engine, dst[first // HALF][:, at : at + width], h[t][:], offsets[:, entries(first, width)])
 
-        def dilate2(t, cells, engine):
-            first, width = cells
-            gather(engine, far2[:, t * S + first : t * S + first + width], h[t][:], q2_sb[:, entries(first, width)])
+        most = {}
 
-        def first_max(t, cells):
-            first, width = cells
-            nc.vector.tensor_tensor(most[:, t * S + first : t * S + first + width], far1[t][:, first : first + width], h[t][:, first : first + width], MAX)
-
-        def by_lines(flat, first, width):
-            return flat[:].rearrange("p (t n i) -> p n t i", t=PACK, i=LINE)[:, first // LINE : (first + width) // LINE, :, :]
+        def first_max(c, tag):
+            first, width = CHUNKS[c]
+            most[c] = shared([P, PACK * width], BF16, "most%d" % c, tag)
+            planes = [far[first // HALF][:].rearrange("p (t n) -> p t n", t=PACK)[:, :, first % HALF : first % HALF + width] for far in (far1, far2)]
+            nc.vector.tensor_tensor(most[c][:].rearrange("p (t n) -> p t n", t=PACK), planes[0], planes[1], MAX)
 
         def second_max(c):
             first, width = CHUNKS[c]
             nc.vector.tensor_tensor(
-                z_woven[c][:].rearrange("p (n i t) -> p n t i", i=LINE, t=PACK), by_lines(most, first, width), by_lines(far2, first, width), MAX
+                z_woven[c][:].rearrange("p (n i t) -> p n t i", i=LINE, t=PACK),
+                most[c][:].rearrange("p (t n i) -> p n t i", t=PACK, i=LINE),
+                h_all[:].rearrange("p (t n i) -> p n t i", t=PACK, i=LINE)[:, first // LINE : (first + width) // LINE, :, :],
+                MAX,
             )
 
         z_codes = [held([P, width], U32, "z_codes%d" % c) for c, (first, width) in enumerate(CHUNKS)]
@@ -251,17 +264,14 @@ def tile_picked_opening_none_p_kernel(tc, x_words, x_scales, w1, w2, offs, p1, p
         erode1(0, "vector")
         leave_psum(1)
         erode2(0, "scalar")
+        weave_w2(0, "w2_woven0")
         erode1(1, "vector")
         leave_psum(2)
         first_min(0)
         erode2(1, "scalar")
-        nc.vector.tensor_copy(
-            w2_woven[:].rearrange("p (n i j) -> p n j i", i=LINE, j=PACK),
-            w2_raw[:].rearrange("p j (n i) -> p n j i", i=LINE),
-        )
         leave_psum(3)
-        second_min(0)
         first_min(1)
+        second_min(0)
         erode1(2, "scalar")
         erode1(3, "vector")
         second_min(1)
@@ -270,37 +280,31 @@ def tile_picked_opening_none_p_kernel(tc, x_words, x_scales, w1, w2, offs, p1, p
         erode2(3, "scalar")
         first_min(3)
         second_min(2)
-        nc.vector.quantize_mx(out=w2_codes[:].bitcast(FP8X4), scales=w2_scale[:], in_=w2_woven[:])
+        quantise_w2(0)
         second_min(3)
 
-        dilate1(0, WHOLE, "scalar")
-        dilate1(1, WHOLE, "scalar")
-        dilate2(0, WHOLE, "scalar")
-        dilate2(1, WHOLE, "scalar")
-        dilate1(2, CHUNKS[0], "vector")
-        first_max(0, WHOLE)
-        dilate1(3, CHUNKS[0], "vector")
-        first_max(2, CHUNKS[0])
-        first_max(1, WHOLE)
-        first_max(3, CHUNKS[0])
-        dilate2(2, CHUNKS[0], "scalar")
-        dilate2(3, CHUNKS[0], "scalar")
-        dilate1(3, CHUNKS[1], "vector")
-        dilate1(3, CHUNKS[2], "vector")
+        for cells in ((0, HALF), (HALF, HALF)):
+            for t in (0, 1):
+                dilate(far1, t, cells, q1_sb, "scalar")
+                dilate(far2, t, cells, q2_sb, "scalar")
+        for t in (2, 3):
+            dilate(far1, t, CHUNKS[0], q1_sb, "vector")
+            dilate(far2, t, CHUNKS[0], q2_sb, "vector")
+        weave_w2(1, "near2_3")
+        first_max(0, "most")
+        quantise_w2(1)
         second_max(0)
-        dilate1(2, CHUNKS[1], "scalar")
-        dilate2(2, CHUNKS[1], "scalar")
-        dilate2(3, CHUNKS[1], "scalar")
-        first_max(3, CHUNKS[1])
+        for t in (2, 3):
+            dilate(far1, t, CHUNKS[1], q1_sb, "scalar")
+            dilate(far2, t, CHUNKS[1], q2_sb, "scalar")
+        first_max(1, "most")
+        for t in (2, 3):
+            dilate(far1, t, CHUNKS[2], q1_sb, "scalar")
+            dilate(far2, t, CHUNKS[2], q2_sb, "scalar")
         quantise_z(0)
-        first_max(2, CHUNKS[1])
-        first_max(3, CHUNKS[2])
-        dilate1(2, CHUNKS[2], "scalar")
         second_max(1)
+        first_max(2, "z_woven0")
         second_product(0)
-        dilate2(2, CHUNKS[2], "scalar")
-        dilate2(3, CHUNKS[2], "scalar")
-        first_max(2, CHUNKS[2])
         quantise_z(1)
         second_max(2)
         second_product(1)

@@ -14,6 +14,8 @@ U8 = mybir.dt.uint8
 FP8X4 = mybir.dt.float8_e4m3fn_x4
 MIN = mybir.AluOpType.min
 MAX = mybir.AluOpType.max
+MULT = mybir.AluOpType.mult
+ADD = mybir.AluOpType.add
 COPY = mybir.ActivationFunctionType.Copy
 
 P = 128
@@ -177,14 +179,14 @@ def tile_picked_opening_none_p_kernel(tc, x_words, x_scales, w1, w2, offs, p1, p
         def erode1(t, engine):
             gather(engine, near1[t][:], y[t][:], p1_sb[:])
 
-        def erode2(t, engine):
-            gather(engine, near2[t][:], y[t][:], p2_sb[:])
+        def erode2(t, engine, first=0, width=S):
+            gather(engine, near2[t][:, first : first + width], y[t][:], p2_sb[:, entries(first, width)])
 
         def first_min(t):
-            nc.vector.tensor_tensor(least[t][:], near1[t][:], y[t][:, 0:S], MIN)
+            nc.vector.tensor_tensor(least[t][:], near1[t][:], near2[t][:], MIN)
 
         def second_min(t):
-            nc.vector.tensor_tensor(h[t][:, 0:S], least[t][:], near2[t][:], MIN)
+            nc.vector.tensor_tensor(h[t][:, 0:S], least[t][:], y[t][:, 0:S], MIN)
             nc.sync.dma_start(out=h_all[:, t * S : (t + 1) * S], in_=h[t][:, 0:S])
 
 
@@ -194,9 +196,13 @@ def tile_picked_opening_none_p_kernel(tc, x_words, x_scales, w1, w2, offs, p1, p
 
         def weave_w2(u, tag):
             w2_woven[u] = shared([P, PACK * N // 2], BF16, "w2_woven%d" % u, tag)
-            nc.vector.tensor_copy(
-                w2_woven[u][:].rearrange("p (n i j) -> p n j i", i=LINE, j=PACK),
-                w2_raw[:, :, u * (N // 2) : (u + 1) * (N // 2)].rearrange("p j (n i) -> p n j i", i=LINE),
+            nc.gpsimd.tensor_scalar(
+                w2_woven[u][:].rearrange("p (n j) -> p n j", j=PACK),
+                w2_raw[:, :, u * (N // 2) : (u + 1) * (N // 2)].rearrange("p j n -> p n j"),
+                1.0,
+                0.0,
+                MULT,
+                ADD,
             )
 
         def quantise_w2(u):
@@ -261,26 +267,27 @@ def tile_picked_opening_none_p_kernel(tc, x_words, x_scales, w1, w2, offs, p1, p
                 queue = nc.scalar if c == LAST and b == len(CHUNK_BANKS[c]) - 2 else nc.sync
                 queue.dma_start(out=out_view[:, rows, first : first + width], in_=result[:, rows, :])
 
+        weave_w2(0, "w2_woven0")
+        weave_w2(1, "w2_woven1")
         erode1(0, "vector")
         leave_psum(1)
-        erode2(0, "scalar")
-        weave_w2(0, "w2_woven0")
-        erode1(1, "vector")
         leave_psum(2)
+        erode1(1, "vector")
+        erode2(0, "scalar")
+        erode1(2, "vector")
+        leave_psum(3)
         first_min(0)
         erode2(1, "scalar")
-        leave_psum(3)
-        first_min(1)
         second_min(0)
-        erode1(2, "scalar")
-        erode1(3, "vector")
-        second_min(1)
         erode2(2, "scalar")
+        first_min(1)
+        erode1(3, "scalar")
         first_min(2)
+        second_min(1)
         erode2(3, "scalar")
+        quantise_w2(0)
         first_min(3)
         second_min(2)
-        quantise_w2(0)
         second_min(3)
 
         for cells in ((0, HALF), (HALF, HALF)):
@@ -290,7 +297,6 @@ def tile_picked_opening_none_p_kernel(tc, x_words, x_scales, w1, w2, offs, p1, p
         for t in (2, 3):
             dilate(far1, t, CHUNKS[0], q1_sb, "vector")
             dilate(far2, t, CHUNKS[0], q2_sb, "vector")
-        weave_w2(1, "near2_3")
         first_max(0, "most")
         quantise_w2(1)
         second_max(0)

@@ -121,48 +121,39 @@ def tile_picked_opening_none_p_kernel(tc, x_words, x_scales, w1, w2, offs, p1, p
         nc.vector.tensor_copy(x_scale[:], scale_table[:].indirect(offs_sb[:]))
         quantise_w1(1, 0, "scale_table")
         x_codes = [held([P, S], U32, "x_codes%d" % g) for g in range(PASSES)]
-        for first in (0, HALF):
-            nc.vector.tensor_copy(x_codes[0][:, first : first + HALF], x_table[0][:].indirect(offs_sb[:, entries(first, HALF)]))
-
-        def first_product(acc, t, g, cells):
-            nc.tensor.matmul_mx(
-                out=acc,
-                lhsT=w1_codes[g, t].bitcast(FP8X4),
-                lhsT_scale=w1_scale[g, t],
-                rhs=x_codes[g][:, cells].bitcast(FP8X4),
-                rhs_scale=x_scale[SCALE_ROWS * g : P, cells],
-                start=(g == 0),
-                stop=(g == PASSES - 1),
-            )
-
-        pieces = [
-            (banks[0][:, 0:HALF], slice(0, HALF)),
-            (banks[1][:, 0:QUARTER], slice(HALF, HALF + QUARTER)),
-            (banks[2][:, 0:QUARTER], slice(HALF + QUARTER, S)),
-        ]
-        for acc, cells in pieces:
-            first_product(acc, 0, 0, cells)
-        plane1_bank = banks[len(pieces)]
-        first_product(plane1_bank[:], 1, 0, slice(0, S))
-        plane2_bank = banks[len(pieces) + 1]
-        first_product(plane2_bank[:], 2, 0, slice(0, S))
-        for first in (0, HALF):
-            nc.vector.tensor_copy(x_codes[1][:, first : first + HALF], x_table[1][:].indirect(offs_sb[:, entries(first, HALF)]))
-        quantise_w1(1, 1, "x_table1")
         y = [held([P, WIDE_WINDOW], F32, "y%d" % t) for t in range(PACK)]
-        for (acc, cells), copy in zip(pieces, (nc.scalar.copy, nc.vector.tensor_copy, nc.scalar.copy)):
-            first_product(acc, 0, 1, cells)
-            copy(y[0][:, cells], acc)
-        first_product(plane1_bank[:], 1, 1, slice(0, S))
-        first_product(plane2_bank[:], 2, 1, slice(0, S))
-        for g in range(PASSES):
-            first_product(banks[1][:], 3, g, slice(0, S))
 
+        def half_bank(t, u):
+            return banks[PACK * u + t][:, 0:HALF]
 
-        y_bank = {1: plane1_bank, 2: plane2_bank, 3: banks[1]}
+        def first_product(g, u):
+            cells = slice(u * HALF, (u + 1) * HALF)
+            nc.vector.tensor_copy(x_codes[g][:, cells], x_table[g][:].indirect(offs_sb[:, entries(u * HALF, HALF)]))
+            for t in range(PACK):
+                nc.tensor.matmul_mx(
+                    out=half_bank(t, u),
+                    lhsT=w1_codes[g, t].bitcast(FP8X4),
+                    lhsT_scale=w1_scale[g, t],
+                    rhs=x_codes[g][:, cells].bitcast(FP8X4),
+                    rhs_scale=x_scale[SCALE_ROWS * g : P, cells],
+                    start=(g == 0),
+                    stop=(g == PASSES - 1),
+                )
 
-        def leave_psum(t):
-            nc.scalar.copy(y[t][:, 0:S], y_bank[t][:])
+        for u in range(2):
+            first_product(0, u)
+        quantise_w1(1, 1, "x_table0")
+        for u in range(2):
+            first_product(1, u)
+
+        def leave_psum(t, u, engine):
+            copy = nc.scalar.copy if engine == "scalar" else nc.vector.tensor_copy
+            copy(y[t][:, u * HALF : (u + 1) * HALF], half_bank(t, u))
+
+        for t in range(PACK - 1):
+            leave_psum(t, 0, "scalar")
+        leave_psum(3, 0, "vector")
+        leave_psum(0, 1, "vector")
 
         def gather(engine, dst, window, offsets):
             if engine == "scalar":
@@ -171,13 +162,13 @@ def tile_picked_opening_none_p_kernel(tc, x_words, x_scales, w1, w2, offs, p1, p
                 nc.vector.tensor_copy(dst, window.indirect(offsets))
 
         h = [held([P, S], F32, "h%d" % t) for t in range(PACK)]
-        h_all = held([P, PACK * S], F32, "h_all")
-        near1 = [held([P, S], F32, "near1_%d" % t) for t in range(PACK)]
+        other = held([P, 2 * PACK * HALF], F32, "other")
+        near1 = [shared([P, S], F32, "near1_%d" % t, "near1_%d" % t) for t in range(PACK)]
         near2 = [shared([P, S], F32, "near2_%d" % t, "near2_%d" % t) for t in range(PACK)]
-        least = [held([P, S], F32, "least%d" % t) for t in range(PACK)]
+        least = [shared([P, S], F32, "least%d" % t, "least%d" % t) for t in range(PACK)]
 
-        def erode1(t, engine):
-            gather(engine, near1[t][:], y[t][:], p1_sb[:])
+        def erode1(t, engine, first=0, width=S):
+            gather(engine, near1[t][:, first : first + width], y[t][:], p1_sb[:, entries(first, width)])
 
         def erode2(t, engine, first=0, width=S):
             gather(engine, near2[t][:, first : first + width], y[t][:], p2_sb[:, entries(first, width)])
@@ -187,11 +178,15 @@ def tile_picked_opening_none_p_kernel(tc, x_words, x_scales, w1, w2, offs, p1, p
 
         def second_min(t):
             nc.vector.tensor_tensor(h[t][:, 0:S], least[t][:], y[t][:, 0:S], MIN)
-            nc.sync.dma_start(out=h_all[:, t * S : (t + 1) * S], in_=h[t][:, 0:S])
+            halves = 2 if t < PAIR else 1
+            nc.sync.dma_start(
+                out=other[:].rearrange("p (u t n) -> p u t n", u=2, t=PACK)[:, 0:halves, t, :],
+                in_=h[t][:, 0 : halves * HALF].rearrange("p (u n) -> p u n", u=halves),
+            )
 
 
         w2_woven = {}
-        w2_codes = held([P, N], U32, "w2_codes")
+        w2_codes = {}
         w2_scale = held([P, N], U8, "w2_scale")
 
         def weave_w2(u, tag):
@@ -205,12 +200,13 @@ def tile_picked_opening_none_p_kernel(tc, x_words, x_scales, w1, w2, offs, p1, p
                 ADD,
             )
 
-        def quantise_w2(u):
+        def quantise_w2(u, tag):
             columns = slice(u * (N // 2), (u + 1) * (N // 2))
-            nc.vector.quantize_mx(out=w2_codes[:, columns].bitcast(FP8X4), scales=w2_scale[:, columns], in_=w2_woven[u][:])
+            w2_codes[u] = shared([P, N // 2], U32, "w2_codes%d" % u, tag)
+            nc.vector.quantize_mx(out=w2_codes[u][:].bitcast(FP8X4), scales=w2_scale[:, columns], in_=w2_woven[u][:])
 
-        far1 = [held([P, PACK * HALF], BF16, "far1_%d" % u) for u in range(2)]
-        far2 = [held([P, PACK * HALF], BF16, "far2_%d" % u) for u in range(2)]
+        far1 = [held([P, PACK * HALF], BF16, "far1_0")]
+        far2 = [held([P, PACK * HALF], BF16, "far2_0")]
         z_woven = [shared([P, PACK * width], BF16, "z_woven%d" % c, "z_woven%d" % c) for c, (first, width) in enumerate(CHUNKS)]
         out_view = out.rearrange("(a p) n -> p a n", p=P)
 
@@ -221,26 +217,34 @@ def tile_picked_opening_none_p_kernel(tc, x_words, x_scales, w1, w2, offs, p1, p
 
         most = {}
 
-        def first_max(c, tag):
-            first, width = CHUNKS[c]
-            most[c] = shared([P, PACK * width], BF16, "most%d" % c, tag)
-            planes = [far[first // HALF][:].rearrange("p (t n) -> p t n", t=PACK)[:, :, first % HALF : first % HALF + width] for far in (far1, far2)]
-            nc.vector.tensor_tensor(most[c][:].rearrange("p (t n) -> p t n", t=PACK), planes[0], planes[1], MAX)
+        def both_neighbours(u, pair):
+            columns = slice(pair * PAIR * HALF, (pair + 1) * PAIR * HALF)
+            nc.vector.tensor_tensor(most[u][:, columns], far1[u][:, columns], far2[u][:, columns], MAX)
 
-        def second_max(c):
+        def self_and_first(t):
+            columns = slice(t * HALF, (t + 1) * HALF)
+            nc.vector.tensor_tensor(most[1][:, columns], far1[1][:, columns], h[t][:, HALF:S], MAX)
+
+        def dilate_other(t, c):
             first, width = CHUNKS[c]
+            at = (PACK + t) * HALF + first - HALF
+            gather("scalar", other[:, at : at + width], h[t][:], q2_sb[:, entries(first, width)])
+
+        def second_max(c, at, count):
+            first, width = CHUNKS[c]
+            u, lines = first // HALF, slice((first % HALF + at) // LINE, (first % HALF + at + count) // LINE)
             nc.vector.tensor_tensor(
-                z_woven[c][:].rearrange("p (n i t) -> p n t i", i=LINE, t=PACK),
-                most[c][:].rearrange("p (t n i) -> p n t i", t=PACK, i=LINE),
-                h_all[:].rearrange("p (t n i) -> p n t i", t=PACK, i=LINE)[:, first // LINE : (first + width) // LINE, :, :],
+                z_woven[c][:, PACK * at : PACK * (at + count)].rearrange("p (n i t) -> p n t i", i=LINE, t=PACK),
+                most[u][:].rearrange("p (t n i) -> p n t i", t=PACK, i=LINE)[:, lines, :, :],
+                other[:, u * PACK * HALF : (u + 1) * PACK * HALF].rearrange("p (t n i) -> p n t i", t=PACK, i=LINE)[:, lines, :, :],
                 MAX,
             )
 
         z_codes = [held([P, width], U32, "z_codes%d" % c) for c, (first, width) in enumerate(CHUNKS)]
         z_scale = [held([P, width], U8, "z_scale%d" % c) for c, (first, width) in enumerate(CHUNKS)]
 
-        def quantise_z(c):
-            nc.vector.quantize_mx(out=z_codes[c][:].bitcast(FP8X4), scales=z_scale[c][:], in_=z_woven[c][:])
+        def quantise_z(c, at, count):
+            nc.vector.quantize_mx(out=z_codes[c][:, at : at + count].bitcast(FP8X4), scales=z_scale[c][:, at : at + count], in_=z_woven[c][:, PACK * at : PACK * (at + count)])
 
         def second_product(c):
             first, width = CHUNKS[c]
@@ -251,7 +255,7 @@ def tile_picked_opening_none_p_kernel(tc, x_words, x_scales, w1, w2, offs, p1, p
                     m = b * per_bank + a
                     nc.tensor.matmul_mx(
                         out=banks[bank][:, a * width : (a + 1) * width],
-                        lhsT=w2_codes[:, m * P : (m + 1) * P].bitcast(FP8X4),
+                        lhsT=w2_codes[m // 2][:, m % 2 * P : (m % 2 + 1) * P].bitcast(FP8X4),
                         lhsT_scale=w2_scale[:, m * P : (m + 1) * P],
                         rhs=z_codes[c][:].bitcast(FP8X4),
                         rhs_scale=z_scale[c][:],
@@ -270,49 +274,60 @@ def tile_picked_opening_none_p_kernel(tc, x_words, x_scales, w1, w2, offs, p1, p
         weave_w2(0, "w2_woven0")
         weave_w2(1, "w2_woven1")
         erode1(0, "vector")
-        leave_psum(1)
-        leave_psum(2)
+        leave_psum(1, 1, "scalar")
+        leave_psum(2, 1, "scalar")
         erode1(1, "vector")
         erode2(0, "scalar")
         erode1(2, "vector")
-        leave_psum(3)
+        leave_psum(3, 1, "scalar")
         first_min(0)
         erode2(1, "scalar")
+        first_min(1)
         second_min(0)
         erode2(2, "scalar")
-        first_min(1)
-        erode1(3, "scalar")
         first_min(2)
         second_min(1)
+        erode1(3, "scalar")
         erode2(3, "scalar")
-        quantise_w2(0)
-        first_min(3)
         second_min(2)
+        first_min(3)
+        for t in (0, 1):
+            dilate(far1, t, (0, HALF), q1_sb, "scalar")
+            dilate(far2, t, (0, HALF), q2_sb, "scalar")
+        dilate(far2, 2, (0, HALF), q2_sb, "scalar")
+        far1.append(shared([P, PACK * HALF], BF16, "far1_1", "least1"))
+        far2.append(shared([P, PAIR * HALF], BF16, "far2_1", "least2"))
+        for t in (0, 1):
+            dilate(far1, t, (HALF, HALF), q1_sb, "scalar")
+            dilate(far2, t, (HALF, HALF), q2_sb, "scalar")
+        dilate(far1, 2, CHUNKS[0], q1_sb, "vector")
         second_min(3)
-
-        for cells in ((0, HALF), (HALF, HALF)):
-            for t in (0, 1):
-                dilate(far1, t, cells, q1_sb, "scalar")
-                dilate(far2, t, cells, q2_sb, "scalar")
+        dilate(far1, 3, CHUNKS[0], q1_sb, "vector")
+        dilate(far2, 3, CHUNKS[0], q2_sb, "vector")
         for t in (2, 3):
-            dilate(far1, t, CHUNKS[0], q1_sb, "vector")
-            dilate(far2, t, CHUNKS[0], q2_sb, "vector")
-        first_max(0, "most")
-        quantise_w2(1)
-        second_max(0)
-        for t in (2, 3):
-            dilate(far1, t, CHUNKS[1], q1_sb, "scalar")
-            dilate(far2, t, CHUNKS[1], q2_sb, "scalar")
-        first_max(1, "most")
-        for t in (2, 3):
-            dilate(far1, t, CHUNKS[2], q1_sb, "scalar")
-            dilate(far2, t, CHUNKS[2], q2_sb, "scalar")
-        quantise_z(0)
-        second_max(1)
-        first_max(2, "z_woven0")
+            dilate(far1, t, (HALF, HALF), q1_sb, "scalar")
+        for c in (1, 2):
+            for t in (2, 3):
+                dilate_other(t, c)
+        most[0] = shared([P, PACK * HALF], BF16, "most0", "least3")
+        quantise_w2(0, "near2_3")
+        both_neighbours(0, 0)
+        both_neighbours(0, 1)
+        quantise_w2(1, "near1_3")
+        second_max(0, 0, QUARTER)
+        second_max(0, QUARTER, QUARTER)
+        quantise_z(0, 0, QUARTER)
+        most[1] = shared([P, PACK * HALF], BF16, "most1", "least3")
+        both_neighbours(1, 0)
+        quantise_z(0, QUARTER, QUARTER)
+        self_and_first(2)
+        self_and_first(3)
         second_product(0)
-        quantise_z(1)
-        second_max(2)
+        second_max(1, 0, QUARTER)
+        second_max(2, 0, QUARTER // 2)
+        quantise_z(1, 0, QUARTER)
+        second_max(2, QUARTER // 2, QUARTER // 2)
+        quantise_z(2, 0, QUARTER // 2)
+        quantise_z(2, QUARTER // 2, QUARTER // 2)
         second_product(1)
-        quantise_z(2)
         second_product(2)

@@ -154,6 +154,7 @@ def tile_picked_opening_none_p_kernel(tc, x_words, x_scales, w1, w2, offs, p1, p
             leave_psum(t, 0, "scalar")
         leave_psum(3, 0, "vector")
         leave_psum(0, 1, "vector")
+        leave_psum(1, 1, "vector")
 
         def gather(engine, dst, window, offsets):
             if engine == "scalar":
@@ -174,10 +175,17 @@ def tile_picked_opening_none_p_kernel(tc, x_words, x_scales, w1, w2, offs, p1, p
             gather(engine, near2[t][:, first : first + width], y[t][:], p2_sb[:, entries(first, width)])
 
         def first_min(t):
-            nc.vector.tensor_tensor(least[t][:], near1[t][:], near2[t][:], MIN)
+            if t < PAIR:
+                for u in range(2):
+                    cells = slice(u * HALF, (u + 1) * HALF)
+                    nc.vector.tensor_tensor(least[t][:, cells], near1[t][:, cells], half_bank(t, u), MIN)
+            else:
+                nc.vector.tensor_tensor(least[t][:], near1[t][:], y[t][:, 0:S], MIN)
 
         def second_min(t):
-            nc.vector.tensor_tensor(h[t][:, 0:S], least[t][:], y[t][:, 0:S], MIN)
+            nc.vector.tensor_tensor(h[t][:, 0:S], least[t][:], near2[t][:], MIN)
+            if t == PACK - 1:
+                return
             halves = 2 if t < PAIR else 1
             nc.sync.dma_start(
                 out=other[:].rearrange("p (u t n) -> p u t n", u=2, t=PACK)[:, 0:halves, t, :],
@@ -217,18 +225,18 @@ def tile_picked_opening_none_p_kernel(tc, x_words, x_scales, w1, w2, offs, p1, p
 
         most = {}
 
-        def both_neighbours(u, pair):
-            columns = slice(pair * PAIR * HALF, (pair + 1) * PAIR * HALF)
+        def both_neighbours(u, planes):
+            columns = slice(0, planes * HALF)
             nc.vector.tensor_tensor(most[u][:, columns], far1[u][:, columns], far2[u][:, columns], MAX)
 
-        def self_and_first(t):
+        def self_and_first(u, t):
             columns = slice(t * HALF, (t + 1) * HALF)
-            nc.vector.tensor_tensor(most[1][:, columns], far1[1][:, columns], h[t][:, HALF:S], MAX)
+            nc.vector.tensor_tensor(most[u][:, columns], far1[u][:, columns], h[t][:, u * HALF : (u + 1) * HALF], MAX)
 
-        def dilate_other(t, c):
+        def dilate_other(t, c, engine):
             first, width = CHUNKS[c]
-            at = (PACK + t) * HALF + first - HALF
-            gather("scalar", other[:, at : at + width], h[t][:], q2_sb[:, entries(first, width)])
+            at = (first // HALF * PACK + t) * HALF + first % HALF
+            gather(engine, other[:, at : at + width], h[t][:], q2_sb[:, entries(first, width)])
 
         def second_max(c, at, count):
             first, width = CHUNKS[c]
@@ -264,7 +272,7 @@ def tile_picked_opening_none_p_kernel(tc, x_words, x_scales, w1, w2, offs, p1, p
                     )
                 rows = slice(b * per_bank, (b + 1) * per_bank)
                 staged = result[:, rows, :].rearrange("p a n -> p (a n)")
-                if c == LAST and b % 2 == 1:
+                if (c == 0 and b < 2) or (c == LAST and b % 2 == 1):
                     nc.vector.tensor_copy(staged, banks[bank][:, 0 : per_bank * width])
                 else:
                     nc.scalar.copy(staged, banks[bank][:, 0 : per_bank * width])
@@ -274,7 +282,6 @@ def tile_picked_opening_none_p_kernel(tc, x_words, x_scales, w1, w2, offs, p1, p
         weave_w2(0, "w2_woven0")
         weave_w2(1, "w2_woven1")
         erode1(0, "vector")
-        leave_psum(1, 1, "scalar")
         leave_psum(2, 1, "scalar")
         erode1(1, "vector")
         erode2(0, "scalar")
@@ -289,43 +296,41 @@ def tile_picked_opening_none_p_kernel(tc, x_words, x_scales, w1, w2, offs, p1, p
         second_min(1)
         erode1(3, "scalar")
         erode2(3, "scalar")
-        second_min(2)
         first_min(3)
-        for t in (0, 1):
+        second_min(2)
+        second_min(3)
+        for t in (0, 1, 2):
             dilate(far1, t, (0, HALF), q1_sb, "scalar")
             dilate(far2, t, (0, HALF), q2_sb, "scalar")
-        dilate(far2, 2, (0, HALF), q2_sb, "scalar")
-        far1.append(shared([P, PACK * HALF], BF16, "far1_1", "least1"))
+        far1.append(shared([P, PACK * HALF], BF16, "far1_1", "near2_2"))
         far2.append(shared([P, PAIR * HALF], BF16, "far2_1", "least2"))
         for t in (0, 1):
             dilate(far1, t, (HALF, HALF), q1_sb, "scalar")
             dilate(far2, t, (HALF, HALF), q2_sb, "scalar")
-        dilate(far1, 2, CHUNKS[0], q1_sb, "vector")
-        second_min(3)
+        quantise_w2(0, "least1")
         dilate(far1, 3, CHUNKS[0], q1_sb, "vector")
-        dilate(far2, 3, CHUNKS[0], q2_sb, "vector")
+        dilate_other(3, 0, "vector")
         for t in (2, 3):
             dilate(far1, t, (HALF, HALF), q1_sb, "scalar")
         for c in (1, 2):
             for t in (2, 3):
-                dilate_other(t, c)
+                dilate_other(t, c, "scalar")
         most[0] = shared([P, PACK * HALF], BF16, "most0", "least3")
-        quantise_w2(0, "near2_3")
-        both_neighbours(0, 0)
-        both_neighbours(0, 1)
-        quantise_w2(1, "near1_3")
+        self_and_first(0, 3)
+        both_neighbours(0, 3)
+        quantise_w2(1, "near2_3")
         second_max(0, 0, QUARTER)
         second_max(0, QUARTER, QUARTER)
         quantise_z(0, 0, QUARTER)
         most[1] = shared([P, PACK * HALF], BF16, "most1", "least3")
-        both_neighbours(1, 0)
+        both_neighbours(1, 2)
         quantise_z(0, QUARTER, QUARTER)
-        self_and_first(2)
-        self_and_first(3)
-        second_product(0)
+        self_and_first(1, 2)
+        self_and_first(1, 3)
         second_max(1, 0, QUARTER)
-        second_max(2, 0, QUARTER // 2)
         quantise_z(1, 0, QUARTER)
+        second_product(0)
+        second_max(2, 0, QUARTER // 2)
         second_max(2, QUARTER // 2, QUARTER // 2)
         quantise_z(2, 0, QUARTER // 2)
         quantise_z(2, QUARTER // 2, QUARTER // 2)

@@ -184,8 +184,6 @@ def tile_picked_opening_none_p_kernel(tc, x_words, x_scales, w1, w2, offs, p1, p
 
         def second_min(t):
             nc.vector.tensor_tensor(h[t][:, 0:S], least[t][:], near2[t][:], MIN)
-            if t == PACK - 1:
-                return
             halves = 2 if t < PAIR else 1
             nc.sync.dma_start(
                 out=other[:].rearrange("p (u t n) -> p u t n", u=2, t=PACK)[:, 0:halves, t, :],
@@ -225,8 +223,8 @@ def tile_picked_opening_none_p_kernel(tc, x_words, x_scales, w1, w2, offs, p1, p
 
         most = {}
 
-        def both_neighbours(u, planes):
-            columns = slice(0, planes * HALF)
+        def both_neighbours(u, pair):
+            columns = slice(pair * PAIR * HALF, (pair + 1) * PAIR * HALF)
             nc.vector.tensor_tensor(most[u][:, columns], far1[u][:, columns], far2[u][:, columns], MAX)
 
         def self_and_first(u, t):
@@ -272,7 +270,7 @@ def tile_picked_opening_none_p_kernel(tc, x_words, x_scales, w1, w2, offs, p1, p
                     )
                 rows = slice(b * per_bank, (b + 1) * per_bank)
                 staged = result[:, rows, :].rearrange("p a n -> p (a n)")
-                if (c == 0 and b < 2) or (c == LAST and b % 2 == 1):
+                if c == LAST and b % 2 == 1:
                     nc.vector.tensor_copy(staged, banks[bank][:, 0 : per_bank * width])
                 else:
                     nc.scalar.copy(staged, banks[bank][:, 0 : per_bank * width])
@@ -299,7 +297,7 @@ def tile_picked_opening_none_p_kernel(tc, x_words, x_scales, w1, w2, offs, p1, p
         first_min(3)
         second_min(2)
         second_min(3)
-        for t in (0, 1, 2):
+        for t in (0, 1):
             dilate(far1, t, (0, HALF), q1_sb, "scalar")
             dilate(far2, t, (0, HALF), q2_sb, "scalar")
         far1.append(shared([P, PACK * HALF], BF16, "far1_1", "near2_2"))
@@ -307,23 +305,24 @@ def tile_picked_opening_none_p_kernel(tc, x_words, x_scales, w1, w2, offs, p1, p
         for t in (0, 1):
             dilate(far1, t, (HALF, HALF), q1_sb, "scalar")
             dilate(far2, t, (HALF, HALF), q2_sb, "scalar")
-        quantise_w2(0, "least1")
-        dilate(far1, 3, CHUNKS[0], q1_sb, "vector")
-        dilate_other(3, 0, "vector")
+        for t in (2, 3):
+            dilate(far1, t, CHUNKS[0], q1_sb, "vector")
+            dilate(far2, t, CHUNKS[0], q2_sb, "vector")
         for t in (2, 3):
             dilate(far1, t, (HALF, HALF), q1_sb, "scalar")
         for c in (1, 2):
             for t in (2, 3):
                 dilate_other(t, c, "scalar")
         most[0] = shared([P, PACK * HALF], BF16, "most0", "least3")
-        self_and_first(0, 3)
-        both_neighbours(0, 3)
+        quantise_w2(0, "least1")
+        both_neighbours(0, 0)
+        both_neighbours(0, 1)
         quantise_w2(1, "near2_3")
         second_max(0, 0, QUARTER)
         second_max(0, QUARTER, QUARTER)
         quantise_z(0, 0, QUARTER)
         most[1] = shared([P, PACK * HALF], BF16, "most1", "least3")
-        both_neighbours(1, 2)
+        both_neighbours(1, 0)
         quantise_z(0, QUARTER, QUARTER)
         self_and_first(1, 2)
         self_and_first(1, 3)

@@ -123,38 +123,41 @@ def tile_picked_opening_none_p_kernel(tc, x_words, x_scales, w1, w2, offs, p1, p
         x_codes = [held([P, S], U32, "x_codes%d" % g) for g in range(PASSES)]
         y = [held([P, WIDE_WINDOW], F32, "y%d" % t) for t in range(PACK)]
 
-        def half_bank(t, u):
-            return banks[PACK * u + t][:, 0:HALF]
+        pieces = [(0, 0, HALF), (1, 0, HALF), (2, 0, HALF), (0, HALF, QUARTER), (0, HALF + QUARTER, QUARTER), (1, HALF, HALF), (2, HALF, HALF), (3, 0, S)]
 
-        def first_product(g, u):
+        def pick_words(g, u):
             cells = slice(u * HALF, (u + 1) * HALF)
             nc.vector.tensor_copy(x_codes[g][:, cells], x_table[g][:].indirect(offs_sb[:, entries(u * HALF, HALF)]))
-            for t in range(PACK):
+
+        def first_product(g):
+            for u in range(2):
+                pick_words(g, u)
+            for b, (t, first, width) in enumerate(pieces):
                 nc.tensor.matmul_mx(
-                    out=half_bank(t, u),
+                    out=banks[b][:, 0:width],
                     lhsT=w1_codes[g, t].bitcast(FP8X4),
                     lhsT_scale=w1_scale[g, t],
-                    rhs=x_codes[g][:, cells].bitcast(FP8X4),
-                    rhs_scale=x_scale[SCALE_ROWS * g : P, cells],
+                    rhs=x_codes[g][:, first : first + width].bitcast(FP8X4),
+                    rhs_scale=x_scale[SCALE_ROWS * g : P, first : first + width],
                     start=(g == 0),
                     stop=(g == PASSES - 1),
                 )
 
-        for u in range(2):
-            first_product(0, u)
+        first_product(0)
         quantise_w1(1, 1, "x_table0")
-        for u in range(2):
-            first_product(1, u)
+        first_product(1)
 
-        def leave_psum(t, u, engine):
+        def leave_psum(b, engine):
+            t, first, width = pieces[b]
             copy = nc.scalar.copy if engine == "scalar" else nc.vector.tensor_copy
-            copy(y[t][:, u * HALF : (u + 1) * HALF], half_bank(t, u))
+            copy(y[t][:, first : first + width], banks[b][:, 0:width])
 
-        for t in range(PACK - 1):
-            leave_psum(t, 0, "scalar")
-        leave_psum(3, 0, "vector")
-        leave_psum(0, 1, "vector")
-        leave_psum(1, 1, "vector")
+        leave_psum(0, "scalar")
+        leave_psum(1, "scalar")
+        leave_psum(2, "vector")
+        leave_psum(3, "vector")
+        leave_psum(4, "scalar")
+        leave_psum(5, "vector")
 
         def gather(engine, dst, window, offsets):
             if engine == "scalar":
@@ -175,12 +178,7 @@ def tile_picked_opening_none_p_kernel(tc, x_words, x_scales, w1, w2, offs, p1, p
             gather(engine, near2[t][:, first : first + width], y[t][:], p2_sb[:, entries(first, width)])
 
         def first_min(t):
-            if t < PAIR:
-                for u in range(2):
-                    cells = slice(u * HALF, (u + 1) * HALF)
-                    nc.vector.tensor_tensor(least[t][:, cells], near1[t][:, cells], half_bank(t, u), MIN)
-            else:
-                nc.vector.tensor_tensor(least[t][:], near1[t][:], y[t][:, 0:S], MIN)
+            nc.vector.tensor_tensor(least[t][:], near1[t][:], y[t][:, 0:S], MIN)
 
         def second_min(t):
             nc.vector.tensor_tensor(h[t][:, 0:S], least[t][:], near2[t][:], MIN)
@@ -280,11 +278,11 @@ def tile_picked_opening_none_p_kernel(tc, x_words, x_scales, w1, w2, offs, p1, p
         weave_w2(0, "w2_woven0")
         weave_w2(1, "w2_woven1")
         erode1(0, "vector")
-        leave_psum(2, 1, "scalar")
+        leave_psum(6, "scalar")
         erode1(1, "vector")
         erode2(0, "scalar")
         erode1(2, "vector")
-        leave_psum(3, 1, "scalar")
+        leave_psum(7, "scalar")
         first_min(0)
         erode2(1, "scalar")
         first_min(1)
@@ -300,14 +298,16 @@ def tile_picked_opening_none_p_kernel(tc, x_words, x_scales, w1, w2, offs, p1, p
         for t in (0, 1):
             dilate(far1, t, (0, HALF), q1_sb, "scalar")
             dilate(far2, t, (0, HALF), q2_sb, "scalar")
+        dilate(far2, 2, (QUARTER, QUARTER), q2_sb, "scalar")
         far1.append(shared([P, PACK * HALF], BF16, "far1_1", "near2_2"))
         far2.append(shared([P, PAIR * HALF], BF16, "far2_1", "least2"))
         for t in (0, 1):
             dilate(far1, t, (HALF, HALF), q1_sb, "scalar")
             dilate(far2, t, (HALF, HALF), q2_sb, "scalar")
-        for t in (2, 3):
-            dilate(far1, t, CHUNKS[0], q1_sb, "vector")
-            dilate(far2, t, CHUNKS[0], q2_sb, "vector")
+        dilate(far1, 2, CHUNKS[0], q1_sb, "vector")
+        dilate(far2, 2, (0, QUARTER), q2_sb, "vector")
+        dilate(far1, 3, CHUNKS[0], q1_sb, "vector")
+        dilate(far2, 3, CHUNKS[0], q2_sb, "vector")
         for t in (2, 3):
             dilate(far1, t, (HALF, HALF), q1_sb, "scalar")
         for c in (1, 2):
@@ -326,10 +326,10 @@ def tile_picked_opening_none_p_kernel(tc, x_words, x_scales, w1, w2, offs, p1, p
         quantise_z(0, QUARTER, QUARTER)
         self_and_first(1, 2)
         self_and_first(1, 3)
-        second_max(1, 0, QUARTER)
-        quantise_z(1, 0, QUARTER)
         second_product(0)
+        second_max(1, 0, QUARTER)
         second_max(2, 0, QUARTER // 2)
+        quantise_z(1, 0, QUARTER)
         second_max(2, QUARTER // 2, QUARTER // 2)
         quantise_z(2, 0, QUARTER // 2)
         quantise_z(2, QUARTER // 2, QUARTER // 2)

@@ -84,10 +84,10 @@ def tile_picked_opening_none_p_kernel(tc, x_words, x_scales, w1, w2, offs, p1, p
         for r in range(0, SCALE_ROWS // 2):
             load_scale_rows(r)
         nc.sync.dma_start(offs_sb[:], offs)
-        load_w1(1)
+        load_x(0)
         for r in range(SCALE_ROWS // 2, SCALE_ROWS):
             load_scale_rows(r)
-        load_x(0)
+        load_w1(1)
         load_x(1)
         nc.sync.dma_start(p1_sb[:], p1)
         nc.sync.dma_start(p2_sb[:], p2)
@@ -100,7 +100,7 @@ def tile_picked_opening_none_p_kernel(tc, x_words, x_scales, w1, w2, offs, p1, p
         def round_w1(g, u):
             dealt = w1_raw[g][:].rearrange("p j (m t) -> p m t j", t=PACK)
             w1_woven[g, u] = held([P, PAIR * P * PACK], BF16, "w1_woven%d_%d" % (g, u))
-            copy = nc.scalar.copy if (g, u) == (1, 0) else nc.vector.tensor_copy
+            copy = nc.scalar.copy if (g, u) == (1, 1) else nc.vector.tensor_copy
             copy(w1_woven[g, u][:].rearrange("p (t m j) -> p m t j", t=PAIR, j=PACK), dealt[:, :, PAIR * u : PAIR * (u + 1), :])
 
         def quantise_w1(g, u, tag):
@@ -111,15 +111,12 @@ def tile_picked_opening_none_p_kernel(tc, x_words, x_scales, w1, w2, offs, p1, p
                 w1_codes[g, PAIR * u + e] = codes[:, e * P : (e + 1) * P]
                 w1_scale[g, PAIR * u + e] = scale[:, e * P : (e + 1) * P]
 
-        for g in range(PASSES):
-            for u in range(PACK // PAIR):
-                round_w1(g, u)
+        for u in range(PACK // PAIR):
+            round_w1(0, u)
         quantise_w1(0, 0, "w1_codes0_0")
         quantise_w1(0, 1, "w1_codes0_1")
 
         x_scale = held([P, S], U8, "x_scale")
-        nc.vector.tensor_copy(x_scale[:], scale_table[:].indirect(offs_sb[:]))
-        quantise_w1(1, 0, "scale_table")
         x_codes = [held([P, S], U32, "x_codes%d" % g) for g in range(PASSES)]
         y = [held([P, WIDE_WINDOW], F32, "y%d" % t) for t in range(PACK)]
 
@@ -129,23 +126,33 @@ def tile_picked_opening_none_p_kernel(tc, x_words, x_scales, w1, w2, offs, p1, p
             cells = slice(u * HALF, (u + 1) * HALF)
             nc.vector.tensor_copy(x_codes[g][:, cells], x_table[g][:].indirect(offs_sb[:, entries(u * HALF, HALF)]))
 
-        def first_product(g):
-            for u in range(2):
-                pick_words(g, u)
-            for b, (t, first, width) in enumerate(pieces):
-                nc.tensor.matmul_mx(
-                    out=banks[b][:, 0:width],
-                    lhsT=w1_codes[g, t].bitcast(FP8X4),
-                    lhsT_scale=w1_scale[g, t],
-                    rhs=x_codes[g][:, first : first + width].bitcast(FP8X4),
-                    rhs_scale=x_scale[SCALE_ROWS * g : P, first : first + width],
-                    start=(g == 0),
-                    stop=(g == PASSES - 1),
-                )
+        def product_pass(g, acc, t, first, width, start):
+            nc.tensor.matmul_mx(
+                out=acc,
+                lhsT=w1_codes[g, t].bitcast(FP8X4),
+                lhsT_scale=w1_scale[g, t],
+                rhs=x_codes[g][:, first : first + width].bitcast(FP8X4),
+                rhs_scale=x_scale[SCALE_ROWS * g : P, first : first + width],
+                start=start,
+                stop=(g == PASSES - 1),
+            )
 
-        first_product(0)
-        quantise_w1(1, 1, "x_table0")
-        first_product(1)
+        for u in range(2):
+            pick_words(0, u)
+        for u in range(2):
+            nc.vector.tensor_copy(x_scale[:, u * HALF : (u + 1) * HALF], scale_table[:].indirect(offs_sb[:, entries(u * HALF, HALF)]))
+            for b, (t, first, width) in enumerate(pieces[:-1]):
+                if first // HALF == u:
+                    product_pass(0, banks[b][:, 0:width], t, first, width, True)
+            product_pass(0, banks[len(pieces) - 1][:, u * HALF : (u + 1) * HALF], PACK - 1, u * HALF, HALF, u == 0)
+        for u in range(PACK // PAIR):
+            round_w1(1, u)
+        quantise_w1(1, 0, "w1_codes1_0")
+        quantise_w1(1, 1, "w1_codes1_1")
+        for u in range(2):
+            pick_words(1, u)
+        for b, (t, first, width) in enumerate(pieces):
+            product_pass(1, banks[b][:, 0:width], t, first, width, False)
 
         def leave_psum(b, engine):
             t, first, width = pieces[b]
@@ -209,7 +216,7 @@ def tile_picked_opening_none_p_kernel(tc, x_words, x_scales, w1, w2, offs, p1, p
             w2_codes[u] = shared([P, N // 2], U32, "w2_codes%d" % u, tag)
             nc.vector.quantize_mx(out=w2_codes[u][:].bitcast(FP8X4), scales=w2_scale[:, columns], in_=w2_woven[u][:])
 
-        far1 = [held([P, PACK * HALF], BF16, "far1_0")]
+        far1 = [shared([P, PACK * HALF], BF16, "far1_0", "far1_0")]
         far2 = [held([P, PACK * HALF], BF16, "far2_0")]
         z_woven = [shared([P, PACK * width], BF16, "z_woven%d" % c, "z_woven%d" % c) for c, (first, width) in enumerate(CHUNKS)]
         out_view = out.rearrange("(a p) n -> p a n", p=P)
@@ -225,9 +232,13 @@ def tile_picked_opening_none_p_kernel(tc, x_words, x_scales, w1, w2, offs, p1, p
             columns = slice(pair * PAIR * HALF, (pair + 1) * PAIR * HALF)
             nc.vector.tensor_tensor(most[u][:, columns], far1[u][:, columns], far2[u][:, columns], MAX)
 
-        def self_and_first(u, t):
-            columns = slice(t * HALF, (t + 1) * HALF)
-            nc.vector.tensor_tensor(most[u][:, columns], far1[u][:, columns], h[t][:, u * HALF : (u + 1) * HALF], MAX)
+        def round_high(rounded):
+            for t in range(PAIR, PACK):
+                nc.gpsimd.tensor_scalar(rounded[:, (t - PAIR) * HALF : (t - PAIR + 1) * HALF], h[t][:, HALF:S], 1.0, 0.0, MULT, ADD)
+
+        def self_and_first(rounded):
+            columns = slice(PAIR * HALF, PACK * HALF)
+            nc.vector.tensor_tensor(most[1][:, columns], far1[1][:, columns], rounded[:], MAX)
 
         def dilate_other(t, c, engine):
             first, width = CHUNKS[c]
@@ -295,17 +306,18 @@ def tile_picked_opening_none_p_kernel(tc, x_words, x_scales, w1, w2, offs, p1, p
         first_min(3)
         second_min(2)
         second_min(3)
+        high_rounded = shared([P, PAIR * HALF], BF16, "high_rounded", "near2_3")
+        round_high(high_rounded)
         for t in (0, 1):
             dilate(far1, t, (0, HALF), q1_sb, "scalar")
             dilate(far2, t, (0, HALF), q2_sb, "scalar")
-        dilate(far2, 2, (QUARTER, QUARTER), q2_sb, "scalar")
         far1.append(shared([P, PACK * HALF], BF16, "far1_1", "near2_2"))
         far2.append(shared([P, PAIR * HALF], BF16, "far2_1", "least2"))
         for t in (0, 1):
             dilate(far1, t, (HALF, HALF), q1_sb, "scalar")
             dilate(far2, t, (HALF, HALF), q2_sb, "scalar")
         dilate(far1, 2, CHUNKS[0], q1_sb, "vector")
-        dilate(far2, 2, (0, QUARTER), q2_sb, "vector")
+        dilate(far2, 2, CHUNKS[0], q2_sb, "vector")
         dilate(far1, 3, CHUNKS[0], q1_sb, "vector")
         dilate(far2, 3, CHUNKS[0], q2_sb, "vector")
         for t in (2, 3):
@@ -317,15 +329,14 @@ def tile_picked_opening_none_p_kernel(tc, x_words, x_scales, w1, w2, offs, p1, p
         quantise_w2(0, "least1")
         both_neighbours(0, 0)
         both_neighbours(0, 1)
-        quantise_w2(1, "near2_3")
+        quantise_w2(1, "near1_3")
         second_max(0, 0, QUARTER)
         second_max(0, QUARTER, QUARTER)
         quantise_z(0, 0, QUARTER)
         most[1] = shared([P, PACK * HALF], BF16, "most1", "least3")
         both_neighbours(1, 0)
         quantise_z(0, QUARTER, QUARTER)
-        self_and_first(1, 2)
-        self_and_first(1, 3)
+        self_and_first(high_rounded)
         second_product(0)
         second_max(1, 0, QUARTER)
         second_max(2, 0, QUARTER // 2)

@@ -117,7 +117,7 @@ def tile_picked_opening_none_p_kernel(tc, x_words, x_scales, w1, w2, offs, p1, p
         quantise_w1(0, 1, "w1_codes0_1")
 
         x_scale = held([P, S], U8, "x_scale")
-        x_codes = [held([P, S], U32, "x_codes%d" % g) for g in range(PASSES)]
+        x_codes = [shared([P, S], U32, "x_codes%d" % g, "x_codes%d" % g) for g in range(PASSES)]
         y = [held([P, WIDE_WINDOW], F32, "y%d" % t) for t in range(PACK)]
 
         pieces = [(0, 0, HALF), (1, 0, HALF), (2, 0, HALF), (0, HALF, QUARTER), (0, HALF + QUARTER, QUARTER), (1, HALF, HALF), (2, HALF, HALF), (3, 0, S)]
@@ -185,7 +185,12 @@ def tile_picked_opening_none_p_kernel(tc, x_words, x_scales, w1, w2, offs, p1, p
             gather(engine, near2[t][:, first : first + width], y[t][:], p2_sb[:, entries(first, width)])
 
         def first_min(t):
-            nc.vector.tensor_tensor(least[t][:], near1[t][:], y[t][:, 0:S], MIN)
+            if t == 1:
+                for b, (plane, first, width) in enumerate(pieces):
+                    if plane == t:
+                        nc.vector.tensor_tensor(least[t][:, first : first + width], near1[t][:, first : first + width], banks[b][:, 0:width], MIN)
+            else:
+                nc.vector.tensor_tensor(least[t][:], near1[t][:], y[t][:, 0:S], MIN)
 
         def second_min(t):
             nc.vector.tensor_tensor(h[t][:, 0:S], least[t][:], near2[t][:], MIN)
@@ -286,7 +291,7 @@ def tile_picked_opening_none_p_kernel(tc, x_words, x_scales, w1, w2, offs, p1, p
                 queue = nc.scalar if c == LAST and b == len(CHUNK_BANKS[c]) - 2 else nc.sync
                 queue.dma_start(out=out_view[:, rows, first : first + width], in_=result[:, rows, :])
 
-        weave_w2(0, "w2_woven0")
+        weave_w2(0, "x_codes1")
         weave_w2(1, "w2_woven1")
         erode1(0, "vector")
         leave_psum(6, "scalar")
@@ -294,12 +299,12 @@ def tile_picked_opening_none_p_kernel(tc, x_words, x_scales, w1, w2, offs, p1, p
         erode2(0, "scalar")
         erode1(2, "vector")
         leave_psum(7, "scalar")
-        first_min(0)
-        erode2(1, "scalar")
         first_min(1)
-        second_min(0)
+        erode2(1, "scalar")
+        first_min(0)
         erode2(2, "scalar")
         first_min(2)
+        second_min(0)
         second_min(1)
         erode1(3, "scalar")
         erode2(3, "scalar")

@@ -237,6 +237,11 @@ def tile_picked_opening_none_p_kernel(tc, x_words, x_scales, w1, w2, offs, p1, p
             columns = slice(pair * PAIR * HALF, (pair + 1) * PAIR * HALF)
             nc.vector.tensor_tensor(most[u][:, columns], far1[u][:, columns], far2[u][:, columns], MAX)
 
+        def low_neighbours(c):
+            first, width = CHUNKS[c]
+            views = [tile[:, 0 : PAIR * HALF].rearrange("p (t n) -> p t n", t=PAIR)[:, :, first - HALF : first - HALF + width] for tile in (most[1], far1[1], far2[1])]
+            nc.vector.tensor_tensor(views[0], views[1], views[2], MAX)
+
         def round_high(rounded):
             for t in range(PAIR, PACK):
                 nc.gpsimd.tensor_scalar(rounded[:, (t - PAIR) * HALF : (t - PAIR + 1) * HALF], h[t][:, HALF:S], 1.0, 0.0, MULT, ADD)
@@ -339,9 +344,10 @@ def tile_picked_opening_none_p_kernel(tc, x_words, x_scales, w1, w2, offs, p1, p
         second_max(0, QUARTER, QUARTER)
         quantise_z(0, 0, QUARTER)
         most[1] = shared([P, PACK * HALF], BF16, "most1", "least3")
-        both_neighbours(1, 0)
+        low_neighbours(1)
         quantise_z(0, QUARTER, QUARTER)
         self_and_first(high_rounded)
+        low_neighbours(2)
         second_product(0)
         second_max(1, 0, QUARTER)
         second_max(2, 0, QUARTER // 2)

@@ -25,6 +25,7 @@ K_PASS = P * PACK
 PASSES = K // K_PASS
 QUADRANT = 32
 SCALE_ROWS = 4
+SPREAD = 8
 LIST_COLUMN = 16
 LINE = 4
 HALF, QUARTER = S // 2, S // 4
@@ -71,23 +72,24 @@ def tile_picked_opening_none_p_kernel(tc, x_words, x_scales, w1, w2, offs, p1, p
         def load_x(g):
             nc.sync.dma_start(out=x_table[g][:].bitcast(I32), in_=x_words[g].rearrange("p n t -> p (n t)").bitcast(I32))
 
-        def load_scale_rows(r):
-            for g in range(PASSES):
-                nc.sync.dma_start(
-                    out=scale_table[SCALE_ROWS * g + r : P : QUADRANT, :].bitcast(I32),
-                    in_=x_scales[g, r :: SCALE_ROWS, :].bitcast(I32),
-                )
-
         nc.vector.memset(scale_table[:].bitcast(I32), 0)
         load_w1(0, slice(0, PAIR))
-        load_w1(0, slice(PAIR, PACK))
-        for r in range(0, SCALE_ROWS // 2):
-            load_scale_rows(r)
         nc.sync.dma_start(offs_sb[:], offs)
+        for g in range(PASSES):
+            nc.sync.dma_start(out=scale_table[SCALE_ROWS * g : P : SPREAD, :].bitcast(I32), in_=x_scales[g].bitcast(I32))
+        load_w1(0, slice(PAIR, PACK))
         load_x(0)
-        for r in range(SCALE_ROWS // 2, SCALE_ROWS):
-            load_scale_rows(r)
         load_w1(1)
+        picked_scale = held([P, S], U8, "picked_scale")
+        x_scale = held([P, S], U8, "x_scale")
+        nc.vector.tensor_copy(picked_scale[:], scale_table[:].indirect(offs_sb[:]))
+        nc.vector.tensor_copy(x_scale[:].bitcast(I32), picked_scale[:].bitcast(I32))
+        for g in range(PASSES):
+            for r in range(1, SCALE_ROWS):
+                nc.sync.dma_start(
+                    out=x_scale[SCALE_ROWS * g + r : P : QUADRANT, :].bitcast(I32),
+                    in_=picked_scale[SCALE_ROWS * g + SPREAD * r : P : QUADRANT, :].bitcast(I32),
+                )
         load_x(1)
         nc.sync.dma_start(p1_sb[:], p1)
         nc.sync.dma_start(p2_sb[:], p2)
@@ -116,7 +118,6 @@ def tile_picked_opening_none_p_kernel(tc, x_words, x_scales, w1, w2, offs, p1, p
         quantise_w1(0, 0, "w1_codes0_0")
         quantise_w1(0, 1, "w1_codes0_1")
 
-        x_scale = held([P, S], U8, "x_scale")
         x_codes = [shared([P, S], U32, "x_codes%d" % g, "x_codes%d" % g) for g in range(PASSES)]
         y = [held([P, WIDE_WINDOW], F32, "y%d" % t) for t in range(PACK)]
 
@@ -140,7 +141,6 @@ def tile_picked_opening_none_p_kernel(tc, x_words, x_scales, w1, w2, offs, p1, p
         for u in range(2):
             pick_words(0, u)
         for u in range(2):
-            nc.vector.tensor_copy(x_scale[:, u * HALF : (u + 1) * HALF], scale_table[:].indirect(offs_sb[:, entries(u * HALF, HALF)]))
             for b, (t, first, width) in enumerate(pieces[:-1]):
                 if first // HALF == u:
                     product_pass(0, banks[b][:, 0:width], t, first, width, True)

@@ -27,7 +27,7 @@ QUADRANT = 32
 SCALE_ROWS = 4
 SPREAD = 8
 LIST_COLUMN = 16
-LINE = 4
+LINE = 2
 HALF, QUARTER = S // 2, S // 4
 WIDE_WINDOW = 2 * S
 CHUNKS = ((0, HALF), (HALF, QUARTER), (HALF + QUARTER, QUARTER))

@@ -73,24 +73,26 @@ def tile_picked_opening_none_p_kernel(tc, x_words, x_scales, w1, w2, offs, p1, p
             nc.sync.dma_start(out=x_table[g][:].bitcast(I32), in_=x_words[g].rearrange("p n t -> p (n t)").bitcast(I32))
 
         nc.vector.memset(scale_table[:].bitcast(I32), 0)
-        load_w1(0, slice(0, PAIR))
+        load_w1(0)
         nc.sync.dma_start(offs_sb[:], offs)
-        for g in range(PASSES):
-            nc.sync.dma_start(out=scale_table[SCALE_ROWS * g : P : SPREAD, :].bitcast(I32), in_=x_scales[g].bitcast(I32))
-        load_w1(0, slice(PAIR, PACK))
+        nc.sync.dma_start(out=scale_table[0:P:SCALE_ROWS, :].bitcast(I32), in_=x_scales.rearrange("g i n -> i g n").bitcast(I32))
         load_x(0)
         load_w1(1)
         picked_scale = held([P, S], U8, "picked_scale")
-        x_scale = held([P, S], U8, "x_scale")
+        x_scale = [held([P, S], U8, "x_scale%d" % g) for g in range(PASSES)]
         nc.vector.tensor_copy(picked_scale[:], scale_table[:].indirect(offs_sb[:]))
-        nc.vector.tensor_copy(x_scale[:].bitcast(I32), picked_scale[:].bitcast(I32))
-        for g in range(PASSES):
+
+        def move_scale_rows(g):
+            nc.vector.tensor_copy(x_scale[g][:].bitcast(I32), picked_scale[:].bitcast(I32))
             for r in range(1, SCALE_ROWS):
                 nc.sync.dma_start(
-                    out=x_scale[SCALE_ROWS * g + r : P : QUADRANT, :].bitcast(I32),
+                    out=x_scale[g][SCALE_ROWS * g + r : P : QUADRANT, :].bitcast(I32),
                     in_=picked_scale[SCALE_ROWS * g + SPREAD * r : P : QUADRANT, :].bitcast(I32),
                 )
+
+        move_scale_rows(0)
         load_x(1)
+        move_scale_rows(1)
         nc.sync.dma_start(p1_sb[:], p1)
         nc.sync.dma_start(p2_sb[:], p2)
         nc.sync.dma_start(out=w2_raw[:], in_=w2.rearrange("(p j) n -> p j n", j=PACK))
@@ -101,8 +103,9 @@ def tile_picked_opening_none_p_kernel(tc, x_words, x_scales, w1, w2, offs, p1, p
 
         def round_w1(g, u):
             dealt = w1_raw[g][:].rearrange("p j (m t) -> p m t j", t=PACK)
-            w1_woven[g, u] = held([P, PAIR * P * PACK], BF16, "w1_woven%d_%d" % (g, u))
-            copy = nc.scalar.copy if (g, u) == (1, 1) else nc.vector.tensor_copy
+            name = "w1_woven%d_%d" % (g, u)
+            w1_woven[g, u] = shared([P, PAIR * P * PACK], BF16, name, "scale_table" if (g, u) == (0, 0) else name)
+            copy = nc.scalar.copy if u == 1 else nc.vector.tensor_copy
             copy(w1_woven[g, u][:].rearrange("p (t m j) -> p m t j", t=PAIR, j=PACK), dealt[:, :, PAIR * u : PAIR * (u + 1), :])
 
         def quantise_w1(g, u, tag):
@@ -133,7 +136,7 @@ def tile_picked_opening_none_p_kernel(tc, x_words, x_scales, w1, w2, offs, p1, p
                 lhsT=w1_codes[g, t].bitcast(FP8X4),
                 lhsT_scale=w1_scale[g, t],
                 rhs=x_codes[g][:, first : first + width].bitcast(FP8X4),
-                rhs_scale=x_scale[SCALE_ROWS * g : P, first : first + width],
+                rhs_scale=x_scale[g][SCALE_ROWS * g : P, first : first + width],
                 start=start,
                 stop=(g == PASSES - 1),
             )

@@ -346,6 +346,16 @@ def tile_picked_opening_none_p_kernel(tc, x_words, x_scales, w1, w2, offs, p1, p
         second_max(0, 0, QUARTER)
         second_max(0, QUARTER, QUARTER)
         quantise_z(0, 0, QUARTER)
+        for u in range(2):
+            nc.tensor.matmul_mx(
+                out=banks[PSUM_BANKS - 1][:, u * HALF : (u + 1) * HALF],
+                lhsT=z_codes[0][:, 0:QUARTER].bitcast(FP8X4),
+                lhsT_scale=z_scale[0][:, 0:QUARTER],
+                rhs=w2_codes[u][:].bitcast(FP8X4),
+                rhs_scale=w2_scale[:, u * (N // 2) : (u + 1) * (N // 2)],
+                start=True,
+                stop=True,
+            )
         most[1] = shared([P, PACK * HALF], BF16, "most1", "least3")
         low_neighbours(1)
         quantise_z(0, QUARTER, QUARTER)

@@ -188,12 +188,7 @@ def tile_picked_opening_none_p_kernel(tc, x_words, x_scales, w1, w2, offs, p1, p
             gather(engine, near2[t][:, first : first + width], y[t][:], p2_sb[:, entries(first, width)])
 
         def first_min(t):
-            if t == 1:
-                for b, (plane, first, width) in enumerate(pieces):
-                    if plane == t:
-                        nc.vector.tensor_tensor(least[t][:, first : first + width], near1[t][:, first : first + width], banks[b][:, 0:width], MIN)
-            else:
-                nc.vector.tensor_tensor(least[t][:], near1[t][:], y[t][:, 0:S], MIN)
+            nc.vector.tensor_tensor(least[t][:], near1[t][:], y[t][:, 0:S], MIN)
 
         def second_min(t):
             nc.vector.tensor_tensor(h[t][:, 0:S], least[t][:], near2[t][:], MIN)

@@ -61,7 +61,7 @@ def tile_picked_opening_none_p_kernel(tc, x_words, x_scales, w1, w2, offs, p1, p
         w1_raw = [held([P, PACK, H], F32, "w1_raw%d" % g) for g in range(PASSES)]
         x_table = [shared([P, T], U32, "x_table%d" % g, "x_table%d" % g) for g in range(PASSES)]
         scale_table = shared([P, T], U8, "scale_table", "scale_table")
-        w2_raw = held([P, PACK, N], F32, "w2_raw")
+        w2_raw = [held([P, PACK, N // 2], F32, "w2_raw%d" % u) for u in range(2)]
 
         def load_w1(g, rows=slice(0, PACK)):
             nc.sync.dma_start(
@@ -95,7 +95,8 @@ def tile_picked_opening_none_p_kernel(tc, x_words, x_scales, w1, w2, offs, p1, p
         move_scale_rows(1)
         nc.sync.dma_start(p1_sb[:], p1)
         nc.sync.dma_start(p2_sb[:], p2)
-        nc.sync.dma_start(out=w2_raw[:], in_=w2.rearrange("(p j) n -> p j n", j=PACK))
+        for u in range(2):
+            nc.sync.dma_start(out=w2_raw[u][:], in_=w2.rearrange("(p j) n -> p j n", j=PACK)[:, :, u * (N // 2) : (u + 1) * (N // 2)])
         nc.sync.dma_start(q1_sb[:], q1)
         nc.sync.dma_start(q2_sb[:], q2)
 
@@ -207,7 +208,7 @@ def tile_picked_opening_none_p_kernel(tc, x_words, x_scales, w1, w2, offs, p1, p
             w2_woven[u] = shared([P, PACK * N // 2], BF16, "w2_woven%d" % u, tag)
             nc.gpsimd.tensor_scalar(
                 w2_woven[u][:].rearrange("p (n j) -> p n j", j=PACK),
-                w2_raw[:, :, u * (N // 2) : (u + 1) * (N // 2)].rearrange("p j n -> p n j"),
+                w2_raw[u][:].rearrange("p j n -> p n j"),
                 1.0,
                 0.0,
                 MULT,
@@ -294,7 +295,7 @@ def tile_picked_opening_none_p_kernel(tc, x_words, x_scales, w1, w2, offs, p1, p
                 queue = nc.scalar if c == LAST and b == len(CHUNK_BANKS[c]) - 2 else nc.sync
                 queue.dma_start(out=out_view[:, rows, first : first + width], in_=result[:, rows, :])
 
-        weave_w2(0, "x_codes1")
+        weave_w2(0, "w2_woven0")
         weave_w2(1, "w2_woven1")
         erode1(0, "vector")
         leave_psum(6, "scalar")

from contextlib import ExitStack

import concourse.mybir as mybir

K, T, S, N, H = 1024, 2048, 512, 512, 512
FLOPS = 2 * K * H * S + 2 * H * N * S

F32 = mybir.dt.float32
BF16 = mybir.dt.bfloat16
I32 = mybir.dt.int32
U32 = mybir.dt.uint32
U16 = mybir.dt.uint16
U8 = mybir.dt.uint8
FP8X4 = mybir.dt.float8_e4m3fn_x4
MIN = mybir.AluOpType.min
MAX = mybir.AluOpType.max
MULT = mybir.AluOpType.mult
ADD = mybir.AluOpType.add
COPY = mybir.ActivationFunctionType.Copy

P = 128
PACK = 4
PAIR = 2
K_PASS = P * PACK
PASSES = K // K_PASS
QUADRANT = 32
SCALE_ROWS = 4
SPREAD = 8
LIST_COLUMN = 16
LINE = 2
HALF, QUARTER = S // 2, S // 4
WIDE_WINDOW = 2 * S
CHUNKS = ((0, HALF), (HALF, QUARTER), (HALF + QUARTER, QUARTER))
LAST = len(CHUNKS) - 1
PSUM_BANKS = 8
CHUNK_BANKS = ((0, 1, 2, 3), (4, 5), (6, 7, 0, 1))


def tile_picked_opening_none_p_kernel(tc, x_words, x_scales, w1, w2, offs, p1, p2, q1, q2, out):
    nc = tc.nc
    with ExitStack() as ctx:
        lists = ctx.enter_context(tc.tile_pool(name="lists", bufs=1))
        keep = ctx.enter_context(tc.tile_pool(name="keep", bufs=1))
        psum = ctx.enter_context(tc.psum_pool(name="psum", bufs=1))

        def held(shape, dtype, name):
            return keep.tile(shape, dtype, name=name, align_bytes=64)

        def shared(shape, dtype, name, tag):
            return keep.tile(shape, dtype, name=name, tag=tag, align_bytes=64)

        def list_tile(name):
            return lists.tile([P, S // LIST_COLUMN], U16, name=name)

        def entries(first, count):
            return slice(first // LIST_COLUMN, (first + count) // LIST_COLUMN)

        offs_sb, p1_sb, p2_sb, q1_sb, q2_sb = [list_tile(name) for name in ("offs_sb", "p1_sb", "p2_sb", "q1_sb", "q2_sb")]
        banks = [psum.tile([P, S], F32, name="bank%d" % b) for b in range(PSUM_BANKS)]

        w1_raw = [held([P, PACK, H], F32, "w1_raw%d" % g) for g in range(PASSES)]
        x_table = [shared([P, T], U32, "x_table%d" % g, "x_table%d" % g) for g in range(PASSES)]
        scale_table = shared([P, T], U8, "scale_table", "scale_table")
        w2_raw = [held([P, PACK, N // 2], F32, "w2_raw%d" % u) for u in range(2)]

        def load_w1(g, rows=slice(0, PACK)):
            nc.sync.dma_start(
                out=w1_raw[g][:, rows, :],
                in_=w1[g * K_PASS : (g + 1) * K_PASS, :].rearrange("(p j) n -> p j n", j=PACK)[:, rows, :],
            )

        def load_x(g):
            nc.sync.dma_start(out=x_table[g][:].bitcast(I32), in_=x_words[g].rearrange("p n t -> p (n t)").bitcast(I32))

        nc.vector.memset(scale_table[:].bitcast(I32), 0)
        load_w1(0)
        nc.sync.dma_start(offs_sb[:], offs)
        nc.sync.dma_start(out=scale_table[0:P:SCALE_ROWS, :].bitcast(I32), in_=x_scales.rearrange("g i n -> i g n").bitcast(I32))
        load_x(0)
        load_w1(1)
        picked_scale = held([P, S], U8, "picked_scale")
        x_scale = [held([P, S], U8, "x_scale%d" % g) for g in range(PASSES)]
        nc.vector.tensor_copy(picked_scale[:], scale_table[:].indirect(offs_sb[:]))

        def move_scale_rows(g):
            nc.vector.tensor_copy(x_scale[g][:].bitcast(I32), picked_scale[:].bitcast(I32))
            for r in range(1, SCALE_ROWS):
                nc.sync.dma_start(
                    out=x_scale[g][SCALE_ROWS * g + r : P : QUADRANT, :].bitcast(I32),
                    in_=picked_scale[SCALE_ROWS * g + SPREAD * r : P : QUADRANT, :].bitcast(I32),
                )

        move_scale_rows(0)
        load_x(1)
        move_scale_rows(1)
        nc.sync.dma_start(p1_sb[:], p1)
        nc.sync.dma_start(p2_sb[:], p2)
        for u in range(2):
            nc.sync.dma_start(out=w2_raw[u][:], in_=w2.rearrange("(p j) n -> p j n", j=PACK)[:, :, u * (N // 2) : (u + 1) * (N // 2)])
        nc.sync.dma_start(q1_sb[:], q1)
        nc.sync.dma_start(q2_sb[:], q2)

        w1_woven, w1_codes, w1_scale = {}, {}, {}

        def round_w1(g, u):
            dealt = w1_raw[g][:].rearrange("p j (m t) -> p m t j", t=PACK)
            name = "w1_woven%d_%d" % (g, u)
            w1_woven[g, u] = shared([P, PAIR * P * PACK], BF16, name, "scale_table" if (g, u) == (0, 0) else name)
            copy = nc.scalar.copy if u == 1 else nc.vector.tensor_copy
            copy(w1_woven[g, u][:].rearrange("p (t m j) -> p m t j", t=PAIR, j=PACK), dealt[:, :, PAIR * u : PAIR * (u + 1), :])

        def quantise_w1(g, u, tag):
            codes = shared([P, PAIR * P], U32, "w1_codes%d_%d" % (g, u), tag)
            scale = held([P, PAIR * P], U8, "w1_scale%d_%d" % (g, u))
            nc.vector.quantize_mx(out=codes[:].bitcast(FP8X4), scales=scale[:], in_=w1_woven[g, u][:])
            for e in range(PAIR):
                w1_codes[g, PAIR * u + e] = codes[:, e * P : (e + 1) * P]
                w1_scale[g, PAIR * u + e] = scale[:, e * P : (e + 1) * P]

        for u in range(PACK // PAIR):
            round_w1(0, u)
        quantise_w1(0, 0, "w1_codes0_0")
        quantise_w1(0, 1, "w1_codes0_1")

        x_codes = [shared([P, S], U32, "x_codes%d" % g, "x_codes%d" % g) for g in range(PASSES)]
        y = [held([P, WIDE_WINDOW], F32, "y%d" % t) for t in range(PACK)]

        pieces = [(0, 0, HALF), (1, 0, HALF), (2, 0, HALF), (0, HALF, QUARTER), (0, HALF + QUARTER, QUARTER), (1, HALF, HALF), (2, HALF, HALF), (3, 0, S)]

        def pick_words(g, u):
            cells = slice(u * HALF, (u + 1) * HALF)
            nc.vector.tensor_copy(x_codes[g][:, cells], x_table[g][:].indirect(offs_sb[:, entries(u * HALF, HALF)]))

        def product_pass(g, acc, t, first, width, start):
            nc.tensor.matmul_mx(
                out=acc,
                lhsT=w1_codes[g, t].bitcast(FP8X4),
                lhsT_scale=w1_scale[g, t],
                rhs=x_codes[g][:, first : first + width].bitcast(FP8X4),
                rhs_scale=x_scale[g][SCALE_ROWS * g : P, first : first + width],
                start=start,
                stop=(g == PASSES - 1),
            )

        for u in range(2):
            pick_words(0, u)
        for u in range(2):
            for b, (t, first, width) in enumerate(pieces[:-1]):
                if first // HALF == u:
                    product_pass(0, banks[b][:, 0:width], t, first, width, True)
            product_pass(0, banks[len(pieces) - 1][:, u * HALF : (u + 1) * HALF], PACK - 1, u * HALF, HALF, u == 0)
        for u in range(PACK // PAIR):
            round_w1(1, u)
        quantise_w1(1, 0, "w1_codes1_0")
        quantise_w1(1, 1, "w1_codes1_1")
        for u in range(2):
            pick_words(1, u)
        for b, (t, first, width) in enumerate(pieces):
            product_pass(1, banks[b][:, 0:width], t, first, width, False)

        def leave_psum(b, engine):
            t, first, width = pieces[b]
            copy = nc.scalar.copy if engine == "scalar" else nc.vector.tensor_copy
            copy(y[t][:, first : first + width], banks[b][:, 0:width])

        leave_psum(0, "scalar")
        leave_psum(1, "scalar")
        leave_psum(2, "vector")
        leave_psum(3, "vector")
        leave_psum(4, "scalar")
        leave_psum(5, "vector")

        def gather(engine, dst, window, offsets):
            if engine == "scalar":
                nc.scalar.activation(dst, window.indirect(offsets), COPY)
            else:
                nc.vector.tensor_copy(dst, window.indirect(offsets))

        h = [held([P, S], F32, "h%d" % t) for t in range(PACK)]
        other = held([P, 2 * PACK * HALF], F32, "other")
        near1 = [shared([P, S], F32, "near1_%d" % t, "near1_%d" % t) for t in range(PACK)]
        near2 = [shared([P, S], F32, "near2_%d" % t, "near2_%d" % t) for t in range(PACK)]
        least = [shared([P, S], F32, "least%d" % t, "least%d" % t) for t in range(PACK)]

        def erode1(t, engine, first=0, width=S):
            gather(engine, near1[t][:, first : first + width], y[t][:], p1_sb[:, entries(first, width)])

        def erode2(t, engine, first=0, width=S):
            gather(engine, near2[t][:, first : first + width], y[t][:], p2_sb[:, entries(first, width)])

        def first_min(t):
            nc.vector.tensor_tensor(least[t][:], near1[t][:], y[t][:, 0:S], MIN)

        def second_min(t):
            nc.vector.tensor_tensor(h[t][:, 0:S], least[t][:], near2[t][:], MIN)
            halves = 2 if t < PAIR else 1
            nc.sync.dma_start(
                out=other[:].rearrange("p (u t n) -> p u t n", u=2, t=PACK)[:, 0:halves, t, :],
                in_=h[t][:, 0 : halves * HALF].rearrange("p (u n) -> p u n", u=halves),
            )


        w2_woven = {}
        w2_codes = {}
        w2_scale = held([P, N], U8, "w2_scale")

        def weave_w2(u, tag):
            w2_woven[u] = shared([P, PACK * N // 2], BF16, "w2_woven%d" % u, tag)
            nc.gpsimd.tensor_scalar(
                w2_woven[u][:].rearrange("p (n j) -> p n j", j=PACK),
                w2_raw[u][:].rearrange("p j n -> p n j"),
                1.0,
                0.0,
                MULT,
                ADD,
            )

        def quantise_w2(u, tag):
            columns = slice(u * (N // 2), (u + 1) * (N // 2))
            w2_codes[u] = shared([P, N // 2], U32, "w2_codes%d" % u, tag)
            nc.vector.quantize_mx(out=w2_codes[u][:].bitcast(FP8X4), scales=w2_scale[:, columns], in_=w2_woven[u][:])

        far1 = [shared([P, PACK * HALF], BF16, "far1_0", "far1_0")]
        far2 = [held([P, PACK * HALF], BF16, "far2_0")]
        z_woven = [shared([P, PACK * width], BF16, "z_woven%d" % c, "z_woven%d" % c) for c, (first, width) in enumerate(CHUNKS)]
        out_view = out.rearrange("(a p) n -> p a n", p=P)

        def dilate(dst, t, cells, offsets, engine):
            first, width = cells
            at = t * HALF + first % HALF
            gather(engine, dst[first // HALF][:, at : at + width], h[t][:], offsets[:, entries(first, width)])

        most = {}

        def both_neighbours(u, pair):
            columns = slice(pair * PAIR * HALF, (pair + 1) * PAIR * HALF)
            nc.vector.tensor_tensor(most[u][:, columns], far1[u][:, columns], far2[u][:, columns], MAX)

        def low_neighbours(c):
            first, width = CHUNKS[c]
            views = [tile[:, 0 : PAIR * HALF].rearrange("p (t n) -> p t n", t=PAIR)[:, :, first - HALF : first - HALF + width] for tile in (most[1], far1[1], far2[1])]
            nc.vector.tensor_tensor(views[0], views[1], views[2], MAX)

        def round_high(rounded):
            for t in range(PAIR, PACK):
                nc.gpsimd.tensor_scalar(rounded[:, (t - PAIR) * HALF : (t - PAIR + 1) * HALF], h[t][:, HALF:S], 1.0, 0.0, MULT, ADD)

        def self_and_first(rounded):
            columns = slice(PAIR * HALF, PACK * HALF)
            nc.vector.tensor_tensor(most[1][:, columns], far1[1][:, columns], rounded[:], MAX)

        def dilate_other(t, c, engine):
            first, width = CHUNKS[c]
            at = (first // HALF * PACK + t) * HALF + first % HALF
            gather(engine, other[:, at : at + width], h[t][:], q2_sb[:, entries(first, width)])

        def second_max(c, at, count):
            first, width = CHUNKS[c]
            u, lines = first // HALF, slice((first % HALF + at) // LINE, (first % HALF + at + count) // LINE)
            nc.vector.tensor_tensor(
                z_woven[c][:, PACK * at : PACK * (at + count)].rearrange("p (n i t) -> p n t i", i=LINE, t=PACK),
                most[u][:].rearrange("p (t n i) -> p n t i", t=PACK, i=LINE)[:, lines, :, :],
                other[:, u * PACK * HALF : (u + 1) * PACK * HALF].rearrange("p (t n i) -> p n t i", t=PACK, i=LINE)[:, lines, :, :],
                MAX,
            )

        z_codes = [held([P, width], U32, "z_codes%d" % c) for c, (first, width) in enumerate(CHUNKS)]
        z_scale = [held([P, width], U8, "z_scale%d" % c) for c, (first, width) in enumerate(CHUNKS)]

        def quantise_z(c, at, count):
            nc.vector.quantize_mx(out=z_codes[c][:, at : at + count].bitcast(FP8X4), scales=z_scale[c][:, at : at + count], in_=z_woven[c][:, PACK * at : PACK * (at + count)])

        def second_product(c):
            first, width = CHUNKS[c]
            result = held([P, N // P, width], F32, "result%d" % c)
            per_bank = (N // P) // len(CHUNK_BANKS[c])
            for b, bank in enumerate(CHUNK_BANKS[c]):
                for a in range(per_bank):
                    m = b * per_bank + a
                    nc.tensor.matmul_mx(
                        out=banks[bank][:, a * width : (a + 1) * width],
                        lhsT=w2_codes[m // 2][:, m % 2 * P : (m % 2 + 1) * P].bitcast(FP8X4),
                        lhsT_scale=w2_scale[:, m * P : (m + 1) * P],
                        rhs=z_codes[c][:].bitcast(FP8X4),
                        rhs_scale=z_scale[c][:],
                        start=True,
                        stop=True,
                    )
                rows = slice(b * per_bank, (b + 1) * per_bank)
                staged = result[:, rows, :].rearrange("p a n -> p (a n)")
                if c == LAST and b % 2 == 1:
                    nc.vector.tensor_copy(staged, banks[bank][:, 0 : per_bank * width])
                else:
                    nc.scalar.copy(staged, banks[bank][:, 0 : per_bank * width])
                queue = nc.scalar if c == LAST and b == len(CHUNK_BANKS[c]) - 2 else nc.sync
                queue.dma_start(out=out_view[:, rows, first : first + width], in_=result[:, rows, :])

        weave_w2(0, "w2_woven0")
        weave_w2(1, "w2_woven1")
        erode1(0, "vector")
        leave_psum(6, "scalar")
        erode1(1, "vector")
        erode2(0, "scalar")
        erode1(2, "vector")
        leave_psum(7, "scalar")
        first_min(1)
        erode2(1, "scalar")
        first_min(0)
        erode2(2, "scalar")
        first_min(2)
        second_min(0)
        second_min(1)
        erode1(3, "scalar")
        erode2(3, "scalar")
        first_min(3)
        second_min(2)
        second_min(3)
        high_rounded = shared([P, PAIR * HALF], BF16, "high_rounded", "near2_3")
        round_high(high_rounded)
        for t in (0, 1):
            dilate(far1, t, (0, HALF), q1_sb, "scalar")
            dilate(far2, t, (0, HALF), q2_sb, "scalar")
        far1.append(shared([P, PACK * HALF], BF16, "far1_1", "near2_2"))
        far2.append(shared([P, PAIR * HALF], BF16, "far2_1", "least2"))
        for t in (0, 1):
            dilate(far1, t, (HALF, HALF), q1_sb, "scalar")
            dilate(far2, t, (HALF, HALF), q2_sb, "scalar")
        dilate(far1, 2, CHUNKS[0], q1_sb, "vector")
        dilate(far2, 2, CHUNKS[0], q2_sb, "vector")
        dilate(far1, 3, CHUNKS[0], q1_sb, "vector")
        dilate(far2, 3, CHUNKS[0], q2_sb, "vector")
        for t in (2, 3):
            dilate(far1, t, (HALF, HALF), q1_sb, "scalar")
        for c in (1, 2):
            for t in (2, 3):
                dilate_other(t, c, "scalar")
        most[0] = shared([P, PACK * HALF], BF16, "most0", "least3")
        quantise_w2(0, "least1")
        both_neighbours(0, 0)
        both_neighbours(0, 1)
        quantise_w2(1, "near1_3")
        second_max(0, 0, QUARTER)
        second_max(0, QUARTER, QUARTER)
        quantise_z(0, 0, QUARTER)
        for u in range(2):
            nc.tensor.matmul_mx(
                out=banks[PSUM_BANKS - 1][:, u * HALF : (u + 1) * HALF],
                lhsT=z_codes[0][:, 0:QUARTER].bitcast(FP8X4),
                lhsT_scale=z_scale[0][:, 0:QUARTER],
                rhs=w2_codes[u][:].bitcast(FP8X4),
                rhs_scale=w2_scale[:, u * (N // 2) : (u + 1) * (N // 2)],
                start=True,
                stop=True,
            )
        most[1] = shared([P, PACK * HALF], BF16, "most1", "least3")
        low_neighbours(1)
        quantise_z(0, QUARTER, QUARTER)
        self_and_first(high_rounded)
        low_neighbours(2)
        second_product(0)
        second_max(1, 0, QUARTER)
        second_max(2, 0, QUARTER // 2)
        quantise_z(1, 0, QUARTER)
        second_max(2, QUARTER // 2, QUARTER // 2)
        quantise_z(2, 0, QUARTER // 2)
        quantise_z(2, QUARTER // 2, QUARTER // 2)
        second_product(1)
        second_product(2)
